import numpy as np, ml_dtypes
CORES = [51,54,179,182]
N = 4
BF = ml_dtypes.bfloat16
def gentries(a):
    return np.ascontiguousarray(a.reshape(8, 16, -1).transpose(0, 2, 1)).reshape(8, -1)
def gtable(e):
    e = np.asarray(e); return np.ascontiguousarray(e.reshape(8, -1, 16).transpose(0, 2, 1)).reshape(128, -1).astype(np.int32)
V, P, XC, B, RO = 256, 512, 4096, 8, 3
E = 16 * V
def place_record(n, a, p, t):
    return ((n * (2 * a + 1) >> 4) + n + 37 * p + 77 * t) & (XC - 1)
def seat(rng, ln, key=None, mix=True, pair=False):
    oc = np.full((N, 8, E), P, np.int64); qs = np.full((N, 8, 16 * P), E, np.int64)
    for r in range(N):
        for g in range(8):
            at = np.flatnonzero((np.arange(16) < ln[r, g][:, None]).reshape(-1))
            if pair and g & 1: at = at[np.argsort(2 * np.minimum(at, at ^ (16 * B)) + (at > (at ^ (16 * B))))]
            s = rng.permutation(16 * P) if key is None else np.argsort(key[r, g].reshape(-1))
            s = s[:len(at)]
            if mix: s = rng.permutation(s)
            oc[r, g, at] = s >> 4; qs[r, g, s] = at
    return oc, qs
def put(oc, qs, r, g, s, n):
    b = int(np.flatnonzero(qs[r, g] == n)[0]); m = int(qs[r, g, s])
    qs[r, g, s] = n; qs[r, g, b] = m; oc[r, g, m] = b >> 4; oc[r, g, n] = s >> 4
def aim(w, y, u):
    i = np.arange(1, 16)[:, None]
    w[0] = (u - np.sum(16 * i * w[1:] + np.minimum(w[1:], y[1:, None]), axis=0)) & (V - 1)
def pack(x, want, oc, qs, th):
    return {"x": np.ascontiguousarray(x.reshape(N, 128, XC)).astype(np.float32).astype(BF), "want": np.stack([want.reshape(128, P)] * N).astype(np.float32).astype(BF),
            "oc": np.stack([gtable(a) for a in oc]), "qs": np.stack([gtable(a) for a in qs]), "th": np.repeat(th, 16, axis=1).reshape(N, 128, 1).astype(np.int32)}
def goods(rng):
    return rng.integers(0, 256, (N, 8, 16, XC)), rng.integers(0, 256, (8, 16, P))
def setup_inputs(rng):
    x, want = goods(rng); oc, qs = seat(rng, rng.integers(8, 17, (N, 8, V)))
    return pack(x, want, oc, qs, rng.integers(450, 901, (N, 8)))
def setup_inputs_alike(rng):
    x, want = goods(rng); ln = rng.choice(np.array([16, 16, 8, 3, 12]), (N, 8, V))
    ln[:, 2] = 16; ln[:, 4] = rng.integers(12, 16, (N, V)); ln[:, 6] = rng.integers(12, 16, (N, V)); ln[:, 6, 1] = 16; ln[N - 1, 6, V - 1] = 15
    key = rng.random((N, 8, P, 1)) + 0.0001 * rng.random((N, 8, P, 16))
    oc, qs = seat(rng, ln, key, False, True)
    want[3] = want[3][:, :1]; x[N - 1, 5] = x[N - 1, 5] >> 1
    key = rng.random((N, 8, P, 16)); one = np.arange(16) == rng.integers(0, 16, (N, P, 1))
    key[:, 4] = np.where(one, -1, np.where(np.roll(one, 1, axis=2), 9, key[:, 4]))
    key[:, 6, 1:N + 1] = 9; key[:, 6, P - 1] = 9; key[N - 1, 6, P - 1, :15] = -1
    for r in range(N): key[r, 6, r + 1, r] = -1
    oc2, qs2 = seat(rng, ln, key)
    oc[:, 2:7:2] = oc2[:, 2:7:2]; qs[:, 2:7:2] = qs2[:, 2:7:2]
    n = np.arange(E); m = n ^ (16 * B)
    for r in range(N):
        a = np.where((n & 15) == 0, n >> 4, np.roll(oc[r, 2], 1)); c = place_record(m, a[m], oc[r, 2], 0)
        y = x[r, 2] >> 1; y[:, c] = y[:, c] | 128; x[r, 2] = y
        put(oc, qs, r, 6, 16 * (r + 1) + r, 128)
    for k in range(15): put(oc, qs, N - 1, 6, 16 * (P - 1) + k, E - 16 + k)
    y = rng.integers(0, 256, 16); y[0] = 255; x[:, 4] = y[:, None]; want[4] = want[4][:, :1]; aim(want[4], y, 0)
    u = 2 + rng.integers(0, V - 3, P); u[1:N + 1] = 1; u[P - 1] = V - 1
    x[:, 6] = 255; aim(want[6], np.full(16, 255), u)
    th = rng.integers(600, 1500, (N, 8)); th[:, 2] = 4080
    return pack(x, want, oc, qs, th)
def setup_inputs_ties(rng):
    x, want = goods(rng); x = 85 * (x >> 6); want = 85 * (want >> 6)
    oc, qs = seat(rng, rng.integers(8, 17, (N, 8, V)))
    for a in (x, oc, qs): a[:, ::2] = a[:1, ::2]
    x[0, 2] = np.minimum(x[0, 2], 170); x[0, 6] = np.minimum(x[0, 6], 170)
    return pack(x, want, oc, qs, 85 * rng.integers(4, 11, (N, 8)) - rng.integers(0, 2, (N, 8)))
def setup_inputs_corners(rng):
    x, want = goods(rng); ln = rng.choice(np.array([0, 1, 15, 16]), (N, 8, V))
    kind = rng.random((N, 8, 1, XC)); x = np.where(kind < 0.4, 255, np.where(kind < 0.5, 0, x))
    cls = rng.integers(0, 4, (8, 1, P)); kind = rng.random((8, 1, P)); many = np.full((8, 16, P), 255); many[:, 1:2] = 255 - cls
    want = np.where(kind < 0.6, many, np.where(kind < 0.7, 0, want))
    want[7, :, ::16] = 255; want[7, 7, ::16] = 254
    for g in range(8):
        x[:g % N, g, 0] = np.minimum(x[:g % N, g, 0], 254)
        for c in range(4): ln[:, g, (16 * 120 * 255 + 4080 - 17 * c) & (V - 1)] = (15, 0, 16, 1)[(g + c) & 3]
    ln[:, 7, V - 1] = 15; ln[:, 0, V - 1] = 16; ln[:, 7, 0] = 16
    c = rng.integers(0, 5, (N, 8, P, 1)); c[:, :, 4::9] = 3
    one = np.arange(16) == rng.integers(0, 16, (N, 8, P, 1))
    key = rng.random((N, 8, P, 1)) + 0.0001 * rng.random((N, 8, P, 16))
    key = key + np.where(c == 0, 0, np.where(c == 1, np.where(one, 3, 0), np.where(c == 2, np.where(one, -3, 3), np.where(c == 3, 6, 1))))
    key[N - 1, 7, 0] = np.where(np.arange(16) < 15, -1, 9)
    oc, qs = seat(rng, ln, key)
    th = rng.choice(np.array([0, 1, 1000, 2000, 4080]), (N, 8)); th[:, ::2] = 4080; th[:, 5] = 4079; th[:, 7] = 4080
    return pack(x, want, oc, qs, th)
def setup_inputs_ends(rng):
    v = np.arange(V); low = np.minimum(v, v ^ B)
    ln = np.where((rng.random((N, 8, V)) < 0.35)[..., low], 16, 0)
    for q in (0, V - 1): ln[..., q] = 16; ln[..., q ^ B] = 16
    who = rng.random((N, 8, P, 1)); who[:, :, 0] = -1; who[:, :, P - 1] = -1
    oc, qs = seat(rng, ln, who + 0.0001 * rng.random((N, 8, P, 16)))
    kind = rng.random((8, 1, P)); want = np.where(kind < 0.25, 255, np.where(kind < 0.4, 0, 255 * rng.integers(0, 2, (8, 16, P))))
    want[:, :, 0] = 255; want[:, :, P - 1] = 255; want[:, :, P // 2] = 0; want[:, :, P - 2] = 0
    kind = rng.random((N, 8, 1, XC)); x = np.where(kind < 0.3, 255, np.where(kind < 0.45, 0, 255 * rng.integers(0, 2, (N, 8, 16, XC))))
    x[..., 0] = 255; x[..., XC - 1] = 255
    for r in range(N):
        for g in range(8):
            put(oc, qs, r, g, 16 * P - 1, E - 1); put(oc, qs, r, g, 0, 0)
            x[r, g, :, int(place_record(E - 1, int(oc[r, g, E - 2]), P - 1, 0))] = 255
    th = np.where(rng.random((N, 8)) < 0.3, 0, 4080); th[:, 0] = 4080; th[:, 1] = 0; th[:, 7] = 4080
    return pack(x, want, oc, qs, th)
def setup_inputs_spread(rng):
    x = np.minimum((np.exp2(8 * rng.random((N, 8, 1, XC))) * rng.random((N, 8, 16, XC))).astype(np.int64), 255)
    want = np.minimum((np.exp2(2 + 6 * rng.random((8, 1, P))) * rng.random((8, 16, P))).astype(np.int64), 255)
    ln = np.minimum((17 * rng.random((N, 8, V)) ** rng.choice(np.array([0.3, 0.6, 1.0, 2.0]), (N, 8, 1))).astype(np.int64), 16)
    oc, qs = seat(rng, ln)
    return pack(x, want, oc, qs, np.minimum(np.exp2(12 * rng.random((N, 8))).astype(np.int64), 4080))
def check_inputs(d):
    bad = []
    for k, hi in (("x", 255), ("want", 255), ("oc", P), ("qs", E), ("th", 4080)):
        a = np.asarray(d[k]).astype(np.float64)
        if not np.all((a >= 0) & (a <= hi)): bad.append("range of " + k)
        elif not np.all(a == np.floor(a)): bad.append("whole numbers of " + k)
    w = np.asarray(d["want"]).astype(np.float32)
    if not np.all(w == w[:1]): bad.append("want alike on all ranks")
    t = np.asarray(d["th"]).reshape(N, 8, 16)
    if not np.all(t == t[:, :, :1]): bad.append("th alike in the rows of a group")
    if "range of oc" in bad or "range of qs" in bad: return bad
    o = np.stack([gentries(a) for a in d["oc"]]).astype(np.int64); q = np.stack([gentries(a) for a in d["qs"]]).astype(np.int64)
    b = (o < P).reshape(N, 8, V, 16)
    if np.any(b[..., 1:] & ~b[..., :-1]): bad.append("queues of oc without gaps")
    ok = True; person = np.arange(16 * P) >> 4
    for r in range(N):
        for g in range(8):
            n = np.bincount(q[r, g], minlength=E + 1)[:E]; back = np.full(E + 1, P, np.int64); back[q[r, g]] = person
            ok = ok and np.array_equal(n, (o[r, g] < P).astype(n.dtype)) and np.array_equal(back[:E], o[r, g])
    if not ok: bad.append("every occupied place of oc in just one slot of qs, of its person")
    return bad
def reference(x, want, oc, qs, th):
    xs = x.astype(np.float32).astype(np.int32).reshape(N, 8, 16, XC); ws = want.astype(np.float32).astype(np.int32).reshape(N, 8, 16, P)
    wp = np.concatenate([ws, np.zeros((N, 8, 16, 1), np.int32)], axis=3); wsum = np.add.reduce(16 * np.arange(16)[:, None] * ws.astype(np.int64), axis=2)
    o = np.stack([gentries(a) for a in oc]).astype(np.int64)
    q = np.stack([gentries(a) for a in qs]).astype(np.int64)
    lim = th.astype(np.int64).reshape(N, 8, 16)[:, :, :1]
    n = np.arange(E); mate = n ^ (16 * B); v = n >> 4; head = (n & 15) == 0; none = np.full((N, 8, 1), E, np.int64)
    for t in range(RO):
        occ = o < P; ahead = np.where(head, v, np.roll(o, 1, axis=2))
        w = np.take_along_axis(wp, o[:, :, None, :], 3)
        own = np.add.reduce(np.minimum(np.take_along_axis(xs, place_record(n, ahead, o, t)[:, :, None, :], 3), w), axis=2).astype(np.int64)
        other = np.add.reduce(np.minimum(np.take_along_axis(xs, place_record(mate, ahead[..., mate], o, t)[:, :, None, :], 3), w), axis=2).astype(np.int64)
        swap = occ & occ[..., mate] & (other + other[..., mate] > own + own[..., mate])
        o2 = np.where(swap, o[..., mate], o); c = np.where(swap, other[..., mate], own)
        qd = np.take_along_axis(np.concatenate([np.where(swap, mate, n), none], axis=2), q, 2)
        best = np.max(np.take_along_axis(np.concatenate([c, np.full((N, 8, 1), -1, np.int64)], axis=2), qd, 2).reshape(N, 8, P, 16), axis=3)
        top = np.max(best, axis=0); holder = np.argmax(best, axis=0)
        tp = np.concatenate([np.broadcast_to(top, (N, 8, P)), np.zeros((N, 8, 1), np.int64)], axis=2)
        go = (c < np.take_along_axis(tp, o2, 2) - lim) | (head & ((v & 7) == t))
        stay = (occ & ~go).astype(np.int64).reshape(N, 8, V, 16)
        to = np.where(stay == 1, 16 * np.arange(V)[:, None] + np.add.accumulate(stay, axis=3) - stay, E).reshape(N, 8, E)
        o = np.full((N, 8, E + 1), P, np.int64); np.put_along_axis(o, to, o2, 2); o = np.ascontiguousarray(o[..., :E])
        q = np.take_along_axis(np.concatenate([to, none], axis=2), qd, 2)
        ln = np.add.reduce(stay, axis=3); empty = q.reshape(N, 8, P, 16) == E; u = (wsum + top) & (V - 1)
        for r in range(N):
            for g in range(8):
                p = np.flatnonzero(np.any(empty[r, g], axis=1) & (top[g] >= 0) & (holder[g] == r)); p = p[ln[r, g, u[r, g, p]] < 16]
                k, i = np.unique(u[r, g, p], return_index=True); p = p[i]; at = 16 * k + ln[r, g, k]
                o[r, g, at] = p; q[r, g, 16 * p + np.argmax(empty[r, g, p], axis=1)] = at
    return {"yoc": np.stack([gtable(a) for a in o]).astype(np.float32), "yq": np.stack([gtable(a) for a in q]).astype(np.float32)}

@@ -1,0 +1,660 @@
+import math
+from concourse.bass import DstId, RemoteDMATransfer
+from concourse.mybir import dt, AluOpType as Op, ActivationFunctionType as Act
+
+LN2 = math.log(2.0)
+BF, F4, FH, I4, U2 = "bfloat16", "float32", "float16", "int32", "uint16"
+WIDTH = {}
+WHERE = {}
+SCRATCH = {}
+
+
+def _decl(dtype, spec):
+    pool, at = "pool_" + dtype, 0
+    for item in spec.split():
+        n, w = item.split(":")
+        WIDTH[n] = int(w)
+        WHERE[n] = (pool, at)
+        at += (int(w) + 15) // 16 * 16
+    SCRATCH[pool] = ("sbuf", [128, at], dtype)
+
+
+_decl(BF, "XT:4096 WT:768 MT:768 T2:528 WG:4096 D0:4096 D1:4096 MG:4096 WD:4096 WN:4096 ZRO:2048 SC0:12288 SC1:12288 FXE:1024 FXO:1024 FN:128 "
+          "EZ:144 EZ4:144 EZS:144 BO:128 IB:128 IBIG:128 TRI:128 PXE:128 PXO:128 PSE:128 PSO:128 RS:8 RW:8 CADD:64 NHI:256 NLO:256 "
+          "FHI:256 FLO:256 XX:512 CMP:512 TT0:512 TT2:512 AH:4336 B0L:512 BL:1024 G2:256 LV:256")
+_decl(FH, "SH2:128 I16:128 I37:128 IX16:128 C1:256 VF:256 KC0:256 KC1:256 KC2:256 O16:256")
+_decl(I4, "OCP:256 QW:528 THI:16 NWI:4096 QI:8 KI:8 B1:8 PI:8 ZI:256 O1:256 T1:256 TQ:256 H:512 HA:512 WSI:32 WSJ:32 TM:32 UH:32 UL:32 PMI:16 "
+          "I2:256 O2:256 BT:256 BT2:256")
+_decl(U2, "OU:256 ZU:256 OCU:256 HU:512 PU:16 OU2:256")
+_decl(F4, "IF:128 BOF:128 TA:128 TB:128 TC:128 TD:128 PA:64 PB:64 PG:8 JB:8 BC:8 G0:8 ONE:256 KC:8 KC16:8 KB:8 Z0:8 ODD:8 EVN:8 THF:8 LIM:8 "
+          "JW0:8 JW1:8 JW:8 PHF:8 NV16:256 NPL:256 C1F:256 HM0:256 HM1:256 HM2:256 HBL:256 Z:256 OE:256 MN:128 TR:128 MC:256 DD:256 PR:128 SW:128 SWD:256 EE:256 "
+          "F:256 SMX:512 PMN:512 RMX:512 RMN:512 R01:512 YN:32 MYK:32 KK:64 K:32 KD:32 KS:512 L4P:32 W4:32 HOLD:32 AP:32 TU:32 LT:128 PEN:128 CK:128 "
+          "RK:128 K1:128 K2:128 KM:128 PM:16 DZ:128 ZS:128 Z2:256 DF:128 FS:128 F2:256 FL:256 Y:256 MV:272 EQ:256 AC:256 APP:256 YO:256 YQ:512 "
+          "LAND0:128 LAND1:128 LAND2:128")
+SCRATCH["OCN"] = ("sbuf", [128, 2, 8, 2, 8], I4)
+SCRATCH["YON"] = ("sbuf", [128, 2, 8, 2, 8], F4)
+for _b in range(8):
+    SCRATCH["P%d" % _b] = ("psum", [128, 512], F4)
+    WIDTH["P%d" % _b] = 512
+    WHERE["P%d" % _b] = ("P%d" % _b, 0)
+SEMAPHORES = (["qv", "qs", "qt", "qg", "sent"] + ["arr%d" % t for t in range(3)] + ["d%d" % i for i in range(24)])
+
+
+def _b(name):
+    return name[0] == "P" and name[1:].isdigit()
+
+
+def rank_program(g, core, T, topo):
+    rank = T.rank_of(core)
+    if rank is None:
+        return
+    Q = {"v": g.vector, "s": g.scalar, "t": g.tensor, "g": g, "y": g.sync}
+    cnt = {}
+    known = {q: {} for q in Q}
+    snap = {}
+    hist = {}
+
+    def A(n, lo=0, hi=None, st=1):
+        hi = WIDTH[n] if hi is None else hi
+        buf, c0 = WHERE[n]
+        ap = T[buf][:, c0 + lo:c0 + hi] if st == 1 else T[buf][:, c0 + lo:c0 + hi:st]
+        return (ap, [(n, lo, hi, st)])
+
+    def clash(a, b):
+        if a[1] <= b[0] or b[1] <= a[0]:
+            return False
+        return (a[0] - b[0]) % math.gcd(a[2], b[2]) == 0
+
+    def IND(win, off):
+        return (win[0].indirect(off[0]), win[1] + off[1])
+
+    def need(q, token):
+        sem, n = token
+        if known[q].get(sem, 0) >= n:
+            return
+        Q[q].wait_ge(T.sem[sem], n)
+        for k2, v2 in snap[token].items():
+            if known[q].get(k2, 0) < v2:
+                known[q][k2] = v2
+        known[q][sem] = n
+
+    def deps(q, reads, writes, dma):
+        toks = []
+        for regs, wr in ((reads, False), (writes, True)):
+            for n, lo, hi, st in regs:
+                bank = _b(n)
+                for (r2, tok, q2, w2, d2) in hist.get(n, []):
+                    if bank and q2 != q:
+                        toks.append(tok)
+                        continue
+                    if not clash((lo, hi, st), r2) or not (w2 or wr):
+                        continue
+                    if q2 == q and not w2 and not dma and not d2:
+                        continue
+                    if q == "t" and q2 == q and tok[1] > cnt.get("qt", 0):
+                        continue
+                    toks.append(tok)
+        best = {}
+        for s, n in toks:
+            best[s] = max(best.get(s, 0), n)
+        for s in sorted(best):
+            need(q, (s, best[s]))
+
+    def note(q, reads, writes, tok, dma):
+        for n, lo, hi, st in reads:
+            hist.setdefault(n, []).append(((lo, hi, st), tok, q, False, dma))
+        for n, lo, hi, st in writes:
+            keep = []
+            for h in hist.get(n, []):
+                covered = st == 1 and lo <= h[0][0] and h[0][1] <= hi or h[0] == (lo, hi, st)
+                if not (covered or _b(n) and h[2] != q):
+                    keep.append(h)
+            hist[n] = keep + [((lo, hi, st), tok, q, True, dma)]
+
+    SEM = {"v": "qv", "s": "qs", "t": "qt", "g": "qg"}
+
+    def run(q, call, reads, writes, inc=True):
+        deps(q, reads, writes, False)
+        sem = SEM[q]
+        inst = call()
+        tok = (sem, cnt.get(sem, 0) + 1)
+        if inc:
+            inst.then_inc(T.sem[sem], 1)
+            cnt[sem] = tok[1]
+            s = dict(known[q])
+            s[sem] = tok[1]
+            snap[tok] = s
+        note(q, reads, writes, tok, False)
+
+    def R(*ops):
+        out = []
+        for o in ops:
+            if isinstance(o, tuple):
+                out += o[1]
+        return out
+
+    def val(o):
+        return o[0] if isinstance(o, tuple) else o
+
+    def tt(o, a, b, op):
+        run("v", lambda: g.vector.tensor_tensor(o[0], a[0], b[0], op), R(a, b), o[1])
+
+    def ts(o, a, s1, op0, s2=None, op1=None):
+        if op1 is None:
+            run("v", lambda: g.vector.tensor_scalar(o[0], a[0], val(s1), None, op0), R(a, s1), o[1])
+        else:
+            run("v", lambda: g.vector.tensor_scalar(o[0], a[0], val(s1), val(s2), op0, op1), R(a, s1, s2), o[1])
+
+    def cp(o, a):
+        run("v", lambda: g.vector.tensor_copy(o[0], a[0]), a[1], o[1])
+
+    def scatter(win, off, a):
+        run("v", lambda: g.vector.tensor_copy(win[0].indirect(off[0]), a[0]), R(a, off), win[1])
+
+    def fill(o, c):
+        run("v", lambda: g.vector.memset(o[0], c), [], o[1])
+
+    def scan(o, d0, d1, init, op0, op1):
+        run("v", lambda: g.vector.tensor_tensor_scan(o[0], d0[0], d1[0], init, op0, op1), R(d0, d1), o[1])
+
+    def act(o, a, func=Act.Copy, bias=0.0, scale=1.0):
+        run("s", lambda: g.scalar.activation(o[0], a[0], func, bias=val(bias), scale=val(scale)), R(a, bias, scale), o[1])
+
+    def mm(o, l, r, start=True, stop=True):
+        run("t", lambda: g.tensor.matmul(o[0], l[0], r[0], start, stop), R(l, r), o[1], inc=stop)
+
+    def mms(o, pairs, start=True, stop=True):
+        for i, (l, r) in enumerate(pairs):
+            mm(o, l, r, start and i == 0, stop and i == len(pairs) - 1)
+
+    def iota(o, pattern, base, cm, small=False):
+        if small:
+            run("g", lambda: g.iota(o[0], pattern, base, cm, allow_small_or_imprecise_dtypes=True), [], o[1])
+        else:
+            run("g", lambda: g.iota(o[0], pattern, base, cm), [], o[1])
+
+    def aff(o, a, pattern, op, fillv, base, cm):
+        run("g", lambda: g.affine_select(o[0], a[0], pattern, op, fillv, base, cm), a[1], o[1])
+
+    ndma = [0]
+
+    def dmas(items):
+        sem = "d%d" % ndma[0]
+        ndma[0] += 1
+        tok = (sem, 16 * len(items))
+        allk = {sem: tok[1]}
+        for q, o, a in items:
+            deps(q, a[1], o[1], True)
+            Q[q].dma_start(o[0], a[0]).then_inc(T.sem[sem], 16)
+            for k2, v2 in known[q].items():
+                allk[k2] = max(allk.get(k2, 0), v2)
+        cnt[sem] = tok[1]
+        snap[tok] = allk
+        for q, o, a in items:
+            note(q, a[1], o[1], tok, True)
+
+    def ext(ap, reg=()):
+        return (ap, list(reg))
+
+    def nat(n, ck):
+        return (T[n][:, ck & 1, :, ck >> 1, :], [(n, 0, 1, 1)])
+
+    dmas([("y", (T.OCN[:], [("OCN", 0, 1, 1)]), ext(T.oc[:]))])
+    dmas([("s", A("QW", 0, 512), ext(T.qs[:]))])
+    dmas([("s", A("WT", 256, 768), ext(T.want[:])), ("s", A("THI", 0, 1), ext(T.th[:]))])
+    dmas([("y", A("OCP", 64 * c, 64 * c + 64), nat("OCN", c)) for c in range(4)])
+    dmas([("y", A("XT", 2048 * c, 2048 * c + 2048), ext(T.x[:, 2048 * c:2048 * c + 2048])) for c in range(2)])
+
+    iota(A("QI", 0, 1), [[0, 1]], 0, 1)
+    for c in range(4):
+        iota(A("NV16", 64 * c, 64 * c + 64), [[256, 8], [16, 8]], 2048 * (c & 1) + 128 * (c >> 1), 0, True)
+    fill(A("ONE"), 1.0)
+    one = A("ONE", 0, 128)
+    aff(A("IF"), one, [[-1, 128]], Op.is_equal, 0.0, 0, 1)
+    aff(A("TA"), one, [[-1, 128]], Op.is_equal, 0.0, 1, 1)
+    aff(A("TB"), one, [[-16, 8], [0, 16]], Op.is_ge, 0.0, 0, 1)
+    aff(A("BOF"), A("TB"), [[16, 8], [0, 16]], Op.is_ge, 0.0, 15, -1)
+    aff(A("PA"), A("ONE", 0, 64), [[-2, 8], [-16, 8]], Op.is_equal, 0.0, 0, 1)
+    aff(A("PB"), A("ONE", 0, 64), [[-2, 8], [-16, 8]], Op.is_equal, 0.0, -1, 1)
+    aff(A("TC"), one, [[-1, 128]], Op.is_equal, 0.0, -1, 1)
+    aff(A("TD"), A("BOF"), [[1, 128]], Op.is_ge, 0.0, -1, -1)
+    aff(A("PG"), A("ONE", 0, 8), [[0, 8]], Op.is_ge, 0.0, -64, 1)
+    iota(A("CK"), [[64, 2], [0, 16], [128, 4]], 0, 0, True)
+    for c in (0, 2, 1, 3):
+        iota(A("NWI", 1024 * c, 1024 * c + 1024), [[256, 8], [16, 8], [1, 16]], 2048 * (c & 1) + 128 * (c >> 1), 0)
+    fill(A("QW", 512, 528), 4096)
+    fill(A("WT", 0, 256), 0.0)
+    fill(A("EZ"), 0.0)
+    fill(A("FXE"), 0.0)
+    fill(A("FXO"), 0.0)
+    fill(A("ZRO"), 0.0)
+
+    def reset(n):
+        dmas([("y", A(n, 4096 + 2048 * c, 6144 + 2048 * c), A("ZRO")) for c in range(4)])
+
+    reset("SC0")
+    reset("SC1")
+    q1, kc, z0 = A("QI", 0, 1), A("KC", 0, 1), A("Z0", 0, 1)
+    ts(A("KI", 0, 1), q1, 15, Op.bitwise_and)
+    cp(kc, A("KI", 0, 1))
+    ts(z0, kc, 0.5, Op.is_lt)
+    ts(A("SH2"), A("TA"), 2.0, Op.mult)
+    fill(A("SH2", 0, 128, 16), 0.0)
+    cp(A("I16"), A("IF"))
+    ts(A("I37"), A("IF"), 37.0, Op.mult)
+    ts(A("IX16"), A("IF"), 16.0, Op.mult)
+    ts(A("NPL"), A("NV16"), kc, Op.add)
+    ts(A("C1F"), A("NV16"), 0.125, Op.mult, 512.0, Op.add)
+    ts(A("C1"), A("C1F"), z0, Op.mult, -511.0, Op.add)
+    ts(A("VF"), A("NV16"), 0.0625, Op.mult)
+    for t in range(3):
+        ts(A("KC%d" % t), A("ONE"), kc, Op.mult, 77.0 * t - 1280.0, Op.add)
+    cp(A("OCU"), A("OCP"))
+    ts(A("OE"), A("OCP"), 511.5, Op.is_lt)
+    ts(A("EE"), A("OCP"), 256.0, Op.add)
+    tt(A("O1"), A("EE"), A("OE"), Op.mult)
+    cp(A("EZ", 15, 143, 16), A("BOF", 0, 128, 16))
+    ts(A("B1", 0, 1), q1, 1, Op.bitwise_and)
+    cp(A("ODD", 0, 1), A("B1", 0, 1))
+    ts(A("EVN", 0, 1), A("ODD", 0, 1), -1.0, Op.mult, 1.0, Op.add)
+    ts(A("KB", 0, 1), kc, 1.5, Op.is_lt)
+    act(A("IB"), A("IF"))
+    act(A("EZ4"), A("EZ"), scale=4.0)
+    act(A("EZS"), A("EZ"), scale=kc)
+    fill(A("CADD"), float(7 - rank))
+
+    npl = A("NPL")
+
+    def ez(n, k):
+        return A(n, 15 - k, 143 - k)
+
+    def lists(t, o16):
+        mms(A("P2", 0, 256), [(A("SH2"), o16), (A("I16"), A("C1"))])
+        kct = A("KC%d" % t)
+        mms(A("P3", 0, 256), [(A("I37"), o16), (A("IX16"), A("VF")), (A("I16"), kct)])
+        for b in range(2):
+            o = A("P3", 256 + 128 * b, 384 + 128 * b)
+            mms(o, [(A("I37"), A("O16", 128 * b, 128 * b + 128)), (A("IX16"), A("VF", 128 - 128 * b, 256 - 128 * b)),
+                    (A("I16"), A("KC%d" % t, 0, 128))])
+        tt(A("T1"), npl, A("P2", 0, 256), Op.mult)
+        ts(A("TQ"), A("T1"), 4, Op.arith_shift_right)
+        tt(A("H", 0, 256), A("TQ"), A("P3", 0, 256), Op.add)
+        ts(A("HA", 0, 256), A("H", 0, 256), 4095, Op.bitwise_and)
+        cp(A("HU", 0, 256), A("HA", 0, 256))
+        for b in range(2):
+            tt(A("H", 256 + 128 * b, 384 + 128 * b), A("TQ", 128 - 128 * b, 256 - 128 * b), A("P3", 256 + 128 * b, 384 + 128 * b), Op.add)
+        ts(A("HA", 256, 512), A("H", 256, 512), 4095, Op.bitwise_and)
+        cp(A("HU", 256, 512), A("HA", 256, 512))
+
+    def persons(first):
+        if not first:
+            ts(A("O1"), A("ZI"), 4, Op.arith_shift_right)
+        cp(A("O16"), A("O1"))
+        cp(A("OU"), A("O1"))
+
+    def wants():
+        for c in (0, 2, 1, 3):
+            act(A("WG", 1024 * c, 1024 * c + 1024), IND(A("WT"), A("OU", 64 * c, 64 * c + 64)))
+
+    def minima(c):
+        w = A("WG", 1024 * c, 1024 * c + 1024)
+        for j, n in ((0, "D0"), (1, "D1")):
+            tt(A(n, 1024 * c, 1024 * c + 1024), IND(A("XT"), A("HU", 256 * j + 64 * c, 256 * j + 64 * c + 64)), w, Op.min)
+        hv, b3 = c & 1, c >> 1
+        for j, n in ((0, "D0"), (1, "D1")):
+            o = A("P%d" % hv, 128 * j + 64 * b3, 128 * j + 64 * b3 + 64)
+            mm(o, A("IB"), A("CADD"), True, False)
+            mms(o, [(ez("EZ4", k), A(n, 1024 * c + k, 1024 * c + 1024 - 15 + k, 16)) for k in range(16)], False, True)
+
+    def slots_gather():
+        for c in (0, 2, 1, 3):
+            tt(A("MG", 1024 * c, 1024 * c + 1024), IND(A("QW"), A("OCU", 64 * c, 64 * c + 64)), A("NWI", 1024 * c, 1024 * c + 1024), Op.is_equal)
+            mms(A("P4", 64 * c, 64 * c + 64), [(ez("EZS", k), A("MG", 1024 * c + k, 1024 * c + 1024 - 15 + k, 16)) for k in range(16)])
+
+    persons(True)
+    lists(0, A("O16"))
+    wants()
+
+    def slots_of_places():
+        ts(A("EE"), A("OCP"), 16.0, Op.mult, 4096.0, Op.add)
+        tt(A("MC"), A("EE"), A("P4", 0, 256), Op.add)
+        tt(A("DD"), A("MC"), A("OE"), Op.mult)
+        tt(A("Z"), A("DD"), npl, Op.max)
+        cp(A("ZI"), A("Z"))
+
+    for n, x, y in (("FXE", "PA", "PB"), ("FXO", "PB", "PA")):
+        cp(A(n, 0, 1024, 16), A(x))
+        cp(A(n, 1, 1024, 16), A(y))
+    act(A("FN"), A("FXE", 0, 128), scale=-1.0)
+    act(A("PXE"), A("IF"), scale=A("EVN", 0, 1))
+    act(A("PXO"), A("IF"), scale=A("ODD", 0, 1))
+    act(A("PSE"), A("TA"), scale=A("EVN", 0, 1))
+    act(A("PSO"), A("TC"), scale=A("ODD", 0, 1))
+    act(A("BO"), A("BOF"))
+    act(A("TRI"), A("TD"))
+    act(A("IBIG"), A("IF"), scale=-33554432.0)
+    act(A("NHI"), A("NV16"), bias=-4096.0)
+    act(A("NLO"), A("ONE"), scale=kc)
+    for c in range(3):
+        w0, w1 = 2048 * c, min(4336, 2048 * c + 2048)
+        act(A("AH", w0, w1), A("ZRO", 0, w1 - w0))
+    for n in ("TT0", "TT2", "KS"):
+        act(A(n), A("ZRO", 0, 512))
+    for t in range(3):
+        act(A("HM%d" % t), A("ZRO", 0, 256))
+    act(A("MV", 256, 272), A("ZRO", 0, 16))
+    act(A("T2", 512, 528), A("ZRO", 0, 16))
+    ts(A("RS"), A("BOF", 0, 128, 16), A("KB", 0, 1), Op.mult)
+    fill(A("RMN"), -1.0e6)
+    fill(A("RMN", 0, 512, 16), 1.0e6)
+    act(A("RMX"), A("RMN"), scale=-1.0)
+
+    def late_constants():
+        ts(A("RW"), A("BOF", 0, 128, 16), kc, Op.mult, 16.0, Op.mult)
+        ts(A("G0"), A("BOF", 0, 128, 16), z0, Op.mult)
+        cp(A("THF", 0, 1), A("THI", 0, 1))
+        ts(A("LIM", 0, 1), A("THF", 0, 1), 4.0, Op.mult, float(rank), Op.add)
+        act(A("TA"), one, scale=A("LIM", 0, 1))
+        for c in range(4):
+            mm(A("P5", 8 * c, 8 * c + 8), A("WT", 256 + 128 * c, 384 + 128 * c), A("RW"))
+        mm(A("P6", 0, 8), A("TA"), A("G0"))
+        for t in range(3):
+            ts(A("HM%d" % t, t, 256, 8), A("ONE", 0, 32), z0, Op.mult, -1.0e6, Op.mult)
+        ts(A("WSI"), A("P5", 0, 32), 255.0, Op.add)
+        for c in range(4):
+            cp(A("L4P", 8 * c, 8 * c + 8), A("P6", 0, 8))
+        ts(A("WSJ"), A("WSI"), 255, Op.bitwise_and)
+        ts(A("W4"), A("WSJ"), 4.0, Op.mult, 32768.0, Op.add)
+        ts(A("KC16", 0, 1), kc, -1.0, Op.mult, 16.0, Op.add)
+        fill(A("MT", 0, 256), 131072.0)
+        fill(A("R01"), 1.0)
+        fill(A("R01", 0, 512, 16), 0.0)
+        fill(A("RK"), -1.0e6)
+        fill(A("RK", 0, 128, 4), 1.0e6)
+        ts(A("CK"), A("CK"), 31.6, Op.add, 2.0 * LN2, Op.mult)
+        w = A("JW", 0, 1)
+        ts(A("B1", 1, 2), q1, -1.0, Op.mult, 127.0, Op.add)
+        for b in range(6):
+            f = A("JB", b, b + 1) if b else w
+            ts(A("PI", b, b + 1), A("B1", 1, 2), b, Op.arith_shift_right, 1, Op.bitwise_and)
+            ts(f, A("PI", b, b + 1), 4.0 ** (2 ** b) - 1.0, Op.mult, 1.0, Op.add)
+            if b:
+                tt(w, w, f, Op.mult)
+        ts(A("JW1", 0, 1), w, A("PG", 0, 1), Op.mult, 2.0 ** -63, Op.mult)
+        ts(A("PHF", 0, 1), A("PG", 0, 1), -1.0, Op.mult, 1.0, Op.add)
+        ts(A("JW0", 0, 1), w, A("PHF", 0, 1), Op.mult, 2.0 ** -63, Op.mult)
+        ts(A("PI", 7, 8), q1, 4, Op.arith_shift_right)
+        ts(A("PHF", 1, 2), A("PI", 7, 8), 256.0, Op.mult)
+        for c in range(4):
+            ts(A("TT2", 128 * c, 128 * c + 128, 16), A("ONE", 0, 8), A("PHF", 1, 2), Op.mult, 4096.0 + 2048.0 * c, Op.add)
+        ts(A("TT2", 1, 512, 16), A("ONE", 0, 32), kc, Op.mult, 16.0, Op.mult)
+        for j in range(4):
+            fill(A("BC", j, j + 1), -2.0 * (2.0 ** (23 - 3 * j)) ** 2)
+        fill(A("BC", 4, 5), -2000.0 * 63.2 * LN2)
+
+    def pair_limits():
+        ts(A("ZU"), A("Z"), 0.0, Op.add)
+        tt(A("MN"), A("Z", 0, 128), A("Z", 128, 256), Op.min)
+        ts(A("TR"), A("MN"), 4095.5, Op.is_lt, 1.0e6, Op.mult)
+
+    def decide(hv):
+        p = "P%d" % hv
+        m, d = A("MC", 128 * hv, 128 * hv + 128), A("DD", 128 * hv, 128 * hv + 128)
+        act(m, A(p, 0, 128))
+        tt(d, A(p, 128, 256), m, Op.subtract)
+        pr, tr = A("PR", 64 * hv, 64 * hv + 64), A("TR", 64 * hv, 64 * hv + 64)
+        tt(pr, A("DD", 128 * hv, 128 * hv + 64), A("DD", 128 * hv + 64, 128 * hv + 128), Op.add)
+        for b in range(2):
+            tt(A("SWD", 128 * hv + 64 * b, 128 * hv + 64 * b + 64), pr, tr, Op.is_gt)
+        tt(A("EE", 128 * hv, 128 * hv + 128), d, A("SWD", 128 * hv, 128 * hv + 128), Op.mult)
+        f = A("F", 128 * hv, 128 * hv + 128)
+        tt(f, A("EE", 128 * hv, 128 * hv + 128), m, Op.add)
+        hi, lo = A("FHI", 128 * hv, 128 * hv + 128), A("FLO", 128 * hv, 128 * hv + 128)
+        act(hi, f)
+        tt(lo, f, hi, Op.subtract)
+        spread(hv, hi, lo)
+
+    def spread(hv, hi, lo):
+        p = "P%d" % (2 + hv)
+        mms(A(p, 0, 128), [(A("PXE"), hi), (A("PSE"), lo)])
+        mms(A(p, 128, 256), [(A("PXO"), hi), (A("PSO"), lo)])
+        act(A("XX", 256 * hv, 256 * hv + 256), A(p, 0, 256))
+
+    ebank = [0]
+
+    def widen(hv, b3, h, dst, heads):
+        p = "P%d" % (4 + ebank[0] % 3)
+        ebank[0] += 1
+        for k in range(16):
+            f = A("FXO" if k & 1 else "FXE", 128 * (k >> 1), 128 * (k >> 1) + 128)
+            x0 = 256 * hv + 128 * (k & 1) + 64 * b3 + 32 * h
+            mm(A(p, k, 512 - 15 + k, 16), f, A("XX", x0, x0 + 32))
+        if heads is not None:
+            x0 = 256 * hv + 64 * b3 + 32 * h
+            mm(A(p, 16 * heads, 512, 128), A("FN"), A("XX", x0 + heads, x0 + 32, 8))
+        j = 1024 * (2 * b3 + hv) + 512 * h
+        act(A(dst, j, j + 512), A(p))
+
+    def put(hv, b3, h, sc, src):
+        c0 = 64 * (2 * b3 + hv) + 32 * h
+        scatter(A(sc), A("ZU", c0, c0 + 32), A(src, 16 * c0, 16 * c0 + 512))
+
+    peers = [d for d in T.cores if d != core]
+    used, plan = [], []
+    for d in sorted(peers, key=lambda d: len(topo.engines(core, d))):
+        es = [e for e in topo.engines(core, d) if e not in used][:4]
+        used += es
+        plan.append((d, sum(1 << e for e in es), len(es)))
+
+    def send(t):
+        own, reg = A("LAND%d" % t, 32 * rank, 32 * rank + 32)
+        deps("g", reg, [], True)
+        tr = []
+        for d, mask, ne in plan:
+            rid, pid = topo.addr(d, core)
+            tr.append(RemoteDMATransfer(dst_ids=[DstId(rid=rid, pnc=pid)], dma_engine_mask=mask, remote_sem=T.sem["arr%d" % t], src=own, dst=own))
+        g.remote_dma_fused(tr, local_sem=T.sem.sent)
+        cnt["sent"] = cnt.get("sent", 0) + sum(p[2] for p in plan)
+        n = sum([p[2] for p in plan])
+        tok = ("arr%d" % t, n)
+        cnt[tok[0]] = n
+        snap[tok] = {tok[0]: n}
+        for r in range(4):
+            if r != rank:
+                hist.setdefault("LAND%d" % t, []).append(((32 * r, 32 * r + 32, 1), tok, "net", True, True))
+
+    def roll(t, sc):
+        for c in range(4):
+            for s in range(16):
+                lo = 4096 + 2048 * c + s
+                mm(A("P7", 128 * c + s, 128 * c + 128 - 15 + s, 16), A(sc, lo, lo + 2048 - 15, 16), A("RS"))
+        scan(A("PMN"), A("RMN"), A("P7"), 0.0, Op.max, Op.min)
+        scan(A("SMX"), A("RMX"), A("P7"), 0.0, Op.min, Op.max)
+        ts(A("YN"), A("PMN", 15, 512, 16), -1.0, Op.mult)
+        key = A("LAND%d" % t, 32 * rank, 32 * rank + 32)
+        tt(key, A("YN"), A("SMX", 15, 512, 16), Op.max)
+        send(t)
+
+    def after_exchange(t):
+        act(A("HBL"), A("HM%d" % t), Act.Identity, bias=A("LIM", 0, 1))
+        for hv in range(2):
+            cp(A("SW", 64 * hv, 64 * hv + 64), A("SWD", 128 * hv, 128 * hv + 64))
+            tt(A("DF", 64 * hv, 64 * hv + 64), A("F", 128 * hv, 128 * hv + 64), A("F", 128 * hv + 64, 128 * hv + 128), Op.subtract)
+        tt(A("DZ"), A("Z", 0, 128), A("Z", 128, 256), Op.subtract)
+        tt(A("ZS"), A("DZ"), A("SW"), Op.mult)
+        tt(A("FS"), A("DF"), A("SW"), Op.mult)
+        tt(A("Z2", 0, 128), A("Z", 0, 128), A("ZS"), Op.subtract)
+        tt(A("Z2", 128, 256), A("Z", 128, 256), A("ZS"), Op.add)
+        cp(A("I2"), A("Z2"))
+        ts(A("O2"), A("I2"), 4, Op.arith_shift_right)
+        cp(A("OU2"), A("O2"))
+        for hv in range(2):
+            tt(A("F2", 64 * hv, 64 * hv + 64), A("F", 128 * hv, 128 * hv + 64), A("FS", 64 * hv, 64 * hv + 64), Op.subtract)
+            tt(A("F2", 128 + 64 * hv, 192 + 64 * hv), A("F", 128 * hv + 64, 128 * hv + 128), A("FS", 64 * hv, 64 * hv + 64), Op.add)
+        tt(A("FL"), A("F2"), A("HBL"), Op.add)
+        ts(A("MYK"), A("LAND%d" % t, 32 * rank, 32 * rank + 32), 0.5, Op.max)
+
+    def thresholds(t):
+        ld = "LAND%d" % t
+        tt(A("KK"), A(ld, 0, 64), A(ld, 64, 128), Op.max)
+        tt(A("K"), A("KK", 0, 32), A("KK", 32, 64), Op.max)
+        cp(A("TT0", 0, 512, 16), A("K"))
+        tt(A("TT0", 1, 512, 16), A("K"), A("TT0", 0, 512, 16), Op.subtract)
+        for c in range(4):
+            mm(A("P0", 128 * c, 128 * c + 128), A("TT0", 128 * c, 128 * c + 128), A("IB"))
+        act(A("MT", 256, 768), A("P0"))
+        for c in range(4):
+            act(A("MG", 1024 * c, 1024 * c + 1024), IND(A("MT"), A("OU2", 64 * c, 64 * c + 64)))
+            mms(A("P1", 64 * c, 64 * c + 64), [(ez("EZ", k), A("MG", 1024 * c + k, 1024 * c + 1024 - 15 + k, 16)) for k in range(16)])
+
+    def applicants():
+        tt(A("KD"), A("K"), A("L4P"), Op.subtract)
+        ts(A("KS", 0, 512, 16), A("KD"), 1.0, Op.max)
+        scan(A("P2"), A("R01"), A("KS"), 0.0, Op.mult, Op.add)
+        tt(A("CMP"), A("PMN"), A("P2"), Op.is_ge)
+        mms(A("P3", 0, 32), [(A("IB"), A("CMP", s, 512 - 15 + s, 16)) for s in range(16)])
+        tt(A("HOLD"), A("K"), A("MYK"), Op.is_equal)
+        tt(A("AP"), A("HOLD"), A("CMP", 15, 512, 16), Op.is_gt)
+        tt(A("TU"), A("K"), A("W4"), Op.add)
+        tt(A("TM"), A("TU"), A("AP"), Op.mult)
+        ts(A("UH"), A("TM"), 2, Op.arith_shift_right, 0x20E8, Op.bitwise_and)
+        ts(A("UL"), A("TM"), 2, Op.arith_shift_right, 0x17, Op.bitwise_and)
+        ts(A("TT2", 2, 512, 16), A("P3", 0, 32), 0.0, Op.add)
+        for c in range(4):
+            mm(A("P7", 128 * c, 128 * c + 128), A("TT2", 128 * c, 128 * c + 128), A("IB"))
+        for x in range(16):
+            v = 0x2000 + 8 * (x >> 3 & 1) + 128 * (x >> 2 & 1) + 64 * (x >> 1 & 1) + 32 * (x & 1)
+            ts(A("AH", 112 + x, 112 + x + 128 * 31 + 1, 128), A("UH"), float(v), Op.is_equal)
+        for y in range(16):
+            v = 16 * (y >> 3 & 1) + (y & 7)
+            ts(A("B0L", 32 * y, 32 * y + 32), A("UL"), float(v), Op.is_equal)
+        for j in range(2):
+            ts(A("BL", 512 * j, 512 * j + 512), A("B0L"), A("JW%d" % j, 0, 1), Op.mult)
+        for c in range(4):
+            for h in range(8):
+                cg = 8 * c + h
+                w0 = 112 + 128 * cg - 16 * h
+                mm(A("P6", c, 128 - 3 + c, 4), A("AH", w0, w0 + 128), A("BL", cg, 1024 - 31 + cg, 32), h == 0, h == 7)
+        act(A("T2", 0, 512), A("P7"))
+        act(A("LT"), A("P6", 0, 128), Act.Ln, bias=2.0 ** -64)
+        act(A("PEN"), A("LT"), Act.Relu, bias=A("BC", 4, 5), scale=-2000.0)
+
+    def winners():
+        tt(A("K1"), A("CK"), A("LT"), Op.subtract)
+        tt(A("K2"), A("K1"), A("PEN"), Op.add)
+        scan(A("KM"), A("RK"), A("K2"), 0.0, Op.max, Op.min)
+        tt(A("PM"), A("KM", 3, 64, 4), A("KM", 67, 128, 4), Op.min)
+        ts(A("PMI"), A("PM"), 0.5 / LN2, Op.mult, 512.0, Op.min)
+        cp(A("PU"), A("PMI"))
+        act(A("G2"), IND(A("T2"), A("PU")))
+        for x in range(16):
+            mm(A("P3", 256 + 16 * x, 272 + 16 * x), A("BO"), A("G2", x, 256 - 15 + x, 16))
+
+    def leave():
+        tt(A("LV"), A("FL"), A("P1", 0, 256), Op.is_lt)
+        for h in range(2):
+            z = A("P4", 256 + 128 * h, 384 + 128 * h)
+            lv = A("LV", 128 * h, 128 * h + 128)
+            mm(A("P4", 128 * h, 128 * h + 128), lv, A("TRI"))
+            mm(z, A("Z2", 128 * h, 128 * h + 128), A("IF"), True, False)
+            mm(z, lv, A("IBIG"), False, True)
+        mm(A("P2", 0, 256), A("BO"), A("LV"))
+        ts(A("BT"), A("P4", 0, 256), float(2 ** 23 + 2 ** 19 + 2 ** 15 + 2 ** 11), Op.mult)
+        ts(A("BT2"), A("BT"), 2 ** 23 + 2 ** 20 + 2 ** 17 + 2 ** 14, Op.bitwise_and)
+        tt(A("Y"), A("BT2"), A("P4", 256, 512), Op.add)
+
+    def close_up(j):
+        th, d = 2.0 ** (23 - 3 * j), 1 << j
+        act(A("P5", 0, 256), A("Y"), Act.Relu, bias=A("BC", j, j + 1), scale=2.0 * th)
+        ts(A("MV", 0, 256), A("Y"), th, Op.subtract, 0.0, Op.max)
+        tt(A("P5", 256, 512), A("Y"), A("P5", 0, 256), Op.subtract)
+        tt(A("Y"), A("P5", 256, 512), A("MV", d, 256 + d), Op.max)
+
+    def settle(last):
+        for h in range(2):
+            mm(A("P0", 128 * h, 128 * h + 128), A("Y", 128 * h, 128 * h + 128), A("IF"))
+        ts(A("EQ"), A("P2", 0, 256), A("KC16", 0, 1), Op.is_equal)
+        tt(A("AC"), A("EQ"), A("P3", 256, 512), Op.mult)
+        tt(A("APP"), A("AC"), npl, Op.max)
+        tt(A("ZI"), A("P0", 0, 256), A("APP"), Op.max)
+
+    def place_numbers():
+        for hv in range(2):
+            p = "P%d" % (2 + hv)
+            for n, (e, f) in ((0, ("PXE", "PSE")), (128, ("PXO", "PSO"))):
+                for b in range(2):
+                    x0 = 128 * b + 64 * hv
+                    mms(A(p, n + 64 * b, n + 64 * b + 64), [(A(e), A("NHI", x0, x0 + 64)), (A(f), A("NLO", x0, x0 + 64))])
+            act(A("XX", 256 * hv, 256 * hv + 256), A(p, 0, 256))
+            for b3 in range(2):
+                for h in range(2):
+                    widen(hv, b3, h, "WN", None)
+
+    for t in range(3):
+        sc = "SC%d" % (t & 1)
+        if t:
+            persons(False)
+            lists(t, A("O16"))
+            wants()
+        minima(0)
+        minima(2)
+        if t == 0:
+            slots_gather()
+            slots_of_places()
+        else:
+            cp(A("Z"), A("ZI"))
+        pair_limits()
+        minima(1)
+        decide(0)
+        minima(3)
+        for b3 in range(2):
+            for h in range(2):
+                widen(0, b3, h, "WD", t)
+        put(0, 0, 0, sc, "WD")
+        put(0, 0, 1, sc, "WD")
+        decide(1)
+        for b3 in range(2):
+            for h in range(2):
+                widen(1, b3, h, "WD", t)
+        put(0, 1, 0, sc, "WD")
+        put(0, 1, 1, sc, "WD")
+        for b3 in range(2):
+            for h in range(2):
+                put(1, b3, h, sc, "WD")
+        if t == 1:
+            place_numbers()
+        roll(t, sc)
+        if t == 0:
+            late_constants()
+        after_exchange(t)
+        thresholds(t)
+        if t:
+            reset("SC%d" % (t - 1 & 1))
+        applicants()
+        leave()
+        close_up(0)
+        winners()
+        for j in range(1, 4):
+            close_up(j)
+        settle(t == 2)
+
+    cp(A("ZU"), A("ZI"))
+    ts(A("O1"), A("ZI"), 4, Op.arith_shift_right)
+    for hv in range(2):
+        for b3 in range(2):
+            for h in range(2):
+                put(hv, b3, h, "SC1", "WN")
+    ts(A("OE"), A("O1"), 255.5, Op.is_lt, 768.0, Op.mult)
+    ts(A("EE"), A("O1"), -256.0, Op.add, 0.0, Op.max)
+    tt(A("AC"), A("EE"), A("OE"), Op.max)
+    ts(A("YO"), A("AC"), 512.0, Op.min)
+    dmas([("s", nat("YON", c), A("YO", 64 * c, 64 * c + 64)) for c in range(4)])
+    dmas([("s", ext(T.yoc[:]), (T.YON[:], [("YON", 0, 1, 1)]))])
+    for h in range(2):
+        p = "P%d" % h
+        mms(A(p, 0, 256), [(ez("EZ", s), A("SC1", 4096 + 4096 * h + s, 8192 + 4096 * h - 15 + s, 16)) for s in range(16)])
+        ts(A("YQ", 256 * h, 256 * h + 256), A(p, 0, 256), 4096.0, Op.add)
+        dmas([("y", ext(T.yq[:, 256 * h:256 * h + 256]), A("YQ", 256 * h, 256 * h + 256))])
+    for s in sorted(cnt):
+        if known["g"].get(s, 0) < cnt[s]:
+            g.wait_ge(T.sem[s], cnt[s])

@@ -19,28 +19,29 @@ def _decl(dtype, spec):
     SCRATCH[pool] = ("sbuf", [128, at], dtype)
 
 
-_decl(BF, "XT:4096 WT:768 MT:768 T2:528 WG:4096 D0:4096 D1:4096 MG:4096 WD:4096 WN:4096 ZRO:2048 SC0:12288 SC1:12288 FXE:1024 FXO:1024 FN:128 "
-          "EZ:144 EZ4:144 EZS:144 BO:128 IB:128 IBIG:128 TRI:128 PXE:128 PXO:128 PSE:128 PSO:128 RS:8 RW:8 CADD:64 NHI:256 NLO:256 "
-          "FHI:256 FLO:256 XX:512 CMP:512 TT0:512 TT2:512 AH:4336 B0L:512 BL:1024 G2:256 LV:256")
-_decl(FH, "SH2:128 I16:128 I37:128 IX16:128 C1:256 VF:256 KC0:256 KC1:256 KC2:256 O16:256")
-_decl(I4, "OCP:256 QW:528 THI:16 NWI:4096 QI:8 KI:8 B1:8 PI:8 ZI:256 O1:256 T1:256 TQ:256 H:512 HA:512 WSI:32 WSJ:32 TM:32 UH:32 UL:32 PMI:16 "
-          "I2:256 O2:256 BT:256 BT2:256")
-_decl(U2, "OU:256 ZU:256 OCU:256 HU:512 PU:16 OU2:256")
-_decl(F4, "IF:128 BOF:128 TA:128 TB:128 TC:128 TD:128 PA:64 PB:64 PG:8 JB:8 BC:8 G0:8 ONE:256 KC:8 KC16:8 KB:8 Z0:8 ODD:8 EVN:8 THF:8 LIM:8 "
-          "JW0:8 JW1:8 JW:8 PHF:8 NV16:256 NPL:256 C1F:256 HM0:256 HM1:256 HM2:256 HBL:256 Z:256 OE:256 MN:128 TR:128 MC:256 DD:256 PR:128 SW:128 SWD:256 EE:256 "
+_decl(BF, "XT:4096 WT:768 MT:768 T2:528 WG:4096 D0:4096 D1:4096 MG:4096 ZRO:2048 WDS:4112 WDE:4112 GS:8192 GE:8448 "
+          "EZ:144 EZ4:144 EZW:144 BO:128 BOP:128 IB:128 IBIG:128 I8K:128 TRI:128 TRQ:128 TRN:128 NLQ:128 NLN:128 "
+          "RS:8 RW:8 CADD:64 FHI:256 FLO:256 EHI:256 ELO:256 CMP:512 TT0:512 TT2:512 AH:4336 B0L:512 BL:1024 G2:256 LV:256 AT:256 "
+          "CQ:256 CN:256")
+_decl(FH, "SH2:128 I16:128 I37:128 IX16:128 C1:256 VF:256 KC0:256 KC1:256 KC2:256 O16:256 O2H:256")
+_decl(I4, "OCP:256 QW:512 THI:16 QI:8 KI:8 B1:8 PI:8 T1:256 TQ:256 H:512 HA:512 W1:512 W2:512 W3:512 W5:512 W6:512 W7:512 W8:512 W9:512 WSI:32 WSJ:32 TM:32 UH:32 UL:32 PMI:16 BT:256 BT2:256")
+_decl(U2, "OU:256 HU:512 PU:16 SU:16 OU2:256 WL:512")
+_decl(F4, "IF:128 BOF:128 TA:128 TB:128 TC:128 TD:128 PA:64 PB:64 PG:8 JB:8 BC:8 G0:8 ONE:256 KC:8 KC16:8 KB:8 KW:8 Z0:8 Z1:8 Z4K:8 ODD:8 EVN:8 THF:8 LIM:8 "
+          "JW0:8 JW1:8 JW:8 PHF:8 NV16:256 NPL:256 NQ:256 WV:256 HV:256 ATQ:256 ATN:256 JC:16 JD:16 C1F:256 HM0:256 HM1:256 HM2:256 HBL:256 "
+          "O:256 OE:256 MN:128 TR:128 MC:256 DD:256 PR:128 SW:128 SWD:256 EE:256 E1:256 DE:128 ES:128 E2:256 E3:256 "
           "F:256 SMX:512 PMN:512 RMX:512 RMN:512 R01:512 YN:32 MYK:32 KK:64 K:32 KD:32 KS:512 L4P:32 W4:32 HOLD:32 AP:32 TU:32 LT:128 PEN:128 CK:128 "
-          "RK:128 K1:128 K2:128 KM:128 PM:16 DZ:128 ZS:128 Z2:256 DF:128 FS:128 F2:256 FL:256 Y:256 MV:272 EQ:256 AC:256 APP:256 YO:256 YQ:512 "
+          "RK:128 K1:128 K2:128 KM:128 PM:16 PF:16 DZ:128 ZS:128 DF:128 FS:128 F2:256 FL:256 Y:256 MV:272 EQ:256 AC:256 YO:256 YQ:512 "
           "LAND0:128 LAND1:128 LAND2:128")
 SCRATCH["OCN"] = ("sbuf", [128, 2, 8, 2, 8], I4)
 SCRATCH["YON"] = ("sbuf", [128, 2, 8, 2, 8], F4)
-for _b in range(8):
-    SCRATCH["P%d" % _b] = ("psum", [128, 512], F4)
-    WIDTH["P%d" % _b] = 512
-    WHERE["P%d" % _b] = ("P%d" % _b, 0)
-SEMAPHORES = (["qv", "qs", "qt", "qg", "sent"] + ["arr%d" % t for t in range(3)] + ["d%d" % i for i in range(24)])
+for _i in range(8):
+    SCRATCH["P%d" % _i] = ("psum", [128, 512], F4)
+    WIDTH["P%d" % _i] = 512
+    WHERE["P%d" % _i] = ("P%d" % _i, 0)
+SEMAPHORES = (["qv", "qs", "qt", "qg", "sent"] + ["arr%d" % t for t in range(3)] + ["d%d" % i for i in range(20)])
 
 
-def _b(name):
+def _bank(name):
     return name[0] == "P" and name[1:].isdigit()
 
 
@@ -49,6 +50,7 @@ def rank_program(g, core, T, topo):
     if rank is None:
         return
     Q = {"v": g.vector, "s": g.scalar, "t": g.tensor, "g": g, "y": g.sync}
+    SEM = {"v": "qv", "s": "qs", "t": "qt", "g": "qg"}
     cnt = {}
     known = {q: {} for q in Q}
     snap = {}
@@ -60,13 +62,17 @@ def rank_program(g, core, T, topo):
         ap = T[buf][:, c0 + lo:c0 + hi] if st == 1 else T[buf][:, c0 + lo:c0 + hi:st]
         return (ap, [(n, lo, hi, st)])
 
+    def ROW(n, i, lo, hi):
+        buf, c0 = WHERE[n]
+        return (T[buf][i:128:16, c0 + lo:c0 + hi], [(n, lo, hi, 1)])
+
+    def IND(win, off):
+        return (win[0].indirect(off[0]), win[1] + off[1])
+
     def clash(a, b):
         if a[1] <= b[0] or b[1] <= a[0]:
             return False
         return (a[0] - b[0]) % math.gcd(a[2], b[2]) == 0
-
-    def IND(win, off):
-        return (win[0].indirect(off[0]), win[1] + off[1])
 
     def need(q, token):
         sem, n = token
@@ -79,24 +85,17 @@ def rank_program(g, core, T, topo):
         known[q][sem] = n
 
     def deps(q, reads, writes, dma):
-        toks = []
+        best = {}
         for regs, wr in ((reads, False), (writes, True)):
             for n, lo, hi, st in regs:
-                bank = _b(n)
+                bank = _bank(n)
                 for (r2, tok, q2, w2, d2) in hist.get(n, []):
-                    if bank and q2 != q:
-                        toks.append(tok)
-                        continue
-                    if not clash((lo, hi, st), r2) or not (w2 or wr):
-                        continue
-                    if q2 == q and not w2 and not dma and not d2:
-                        continue
-                    if q == "t" and q2 == q and tok[1] > cnt.get("qt", 0):
-                        continue
-                    toks.append(tok)
-        best = {}
-        for s, n in toks:
-            best[s] = max(best.get(s, 0), n)
+                    if not (bank and q2 != q):
+                        if not clash((lo, hi, st), r2) or not (w2 or wr):
+                            continue
+                        if q == "t" and q2 == q and tok[1] > cnt.get("qt", 0):
+                            continue
+                    best[tok[0]] = max(best.get(tok[0], 0), tok[1])
         for s in sorted(best):
             need(q, (s, best[s]))
 
@@ -107,11 +106,9 @@ def rank_program(g, core, T, topo):
             keep = []
             for h in hist.get(n, []):
                 covered = st == 1 and lo <= h[0][0] and h[0][1] <= hi or h[0] == (lo, hi, st)
-                if not (covered or _b(n) and h[2] != q):
+                if not (covered or _bank(n) and h[2] != q):
                     keep.append(h)
             hist[n] = keep + [((lo, hi, st), tok, q, True, dma)]
-
-    SEM = {"v": "qv", "s": "qs", "t": "qt", "g": "qg"}
 
     def run(q, call, reads, writes, inc=True):
         deps(q, reads, writes, False)
@@ -200,41 +197,29 @@ def rank_program(g, core, T, topo):
         return (T[n][:, ck & 1, :, ck >> 1, :], [(n, 0, 1, 1)])
 
     dmas([("y", (T.OCN[:], [("OCN", 0, 1, 1)]), ext(T.oc[:]))])
-    dmas([("s", A("QW", 0, 512), ext(T.qs[:]))])
     dmas([("s", A("WT", 256, 768), ext(T.want[:])), ("s", A("THI", 0, 1), ext(T.th[:]))])
     dmas([("y", A("OCP", 64 * c, 64 * c + 64), nat("OCN", c)) for c in range(4)])
     dmas([("y", A("XT", 2048 * c, 2048 * c + 2048), ext(T.x[:, 2048 * c:2048 * c + 2048])) for c in range(2)])
+    dmas([("s", A("QW"), ext(T.qs[:]))])
 
-    iota(A("QI", 0, 1), [[0, 1]], 0, 1)
+    q1, kc, z0, one = A("QI", 0, 1), A("KC", 0, 1), A("Z0", 0, 1), A("ONE", 0, 128)
+    iota(q1, [[0, 1]], 0, 1)
     for c in range(4):
         iota(A("NV16", 64 * c, 64 * c + 64), [[256, 8], [16, 8]], 2048 * (c & 1) + 128 * (c >> 1), 0, True)
     fill(A("ONE"), 1.0)
-    one = A("ONE", 0, 128)
+    fill(A("ZRO"), 0.0)
     aff(A("IF"), one, [[-1, 128]], Op.is_equal, 0.0, 0, 1)
     aff(A("TA"), one, [[-1, 128]], Op.is_equal, 0.0, 1, 1)
     aff(A("TB"), one, [[-16, 8], [0, 16]], Op.is_ge, 0.0, 0, 1)
     aff(A("BOF"), A("TB"), [[16, 8], [0, 16]], Op.is_ge, 0.0, 15, -1)
-    aff(A("PA"), A("ONE", 0, 64), [[-2, 8], [-16, 8]], Op.is_equal, 0.0, 0, 1)
-    aff(A("PB"), A("ONE", 0, 64), [[-2, 8], [-16, 8]], Op.is_equal, 0.0, -1, 1)
-    aff(A("TC"), one, [[-1, 128]], Op.is_equal, 0.0, -1, 1)
     aff(A("TD"), A("BOF"), [[1, 128]], Op.is_ge, 0.0, -1, -1)
     aff(A("PG"), A("ONE", 0, 8), [[0, 8]], Op.is_ge, 0.0, -64, 1)
     iota(A("CK"), [[64, 2], [0, 16], [128, 4]], 0, 0, True)
-    for c in (0, 2, 1, 3):
-        iota(A("NWI", 1024 * c, 1024 * c + 1024), [[256, 8], [16, 8], [1, 16]], 2048 * (c & 1) + 128 * (c >> 1), 0)
-    fill(A("QW", 512, 528), 4096)
+    for c in range(4):
+        iota(A("WV", 64 * c, 64 * c + 64), [[1, 64]], 2048 * (c & 1) + 64 * (c >> 1), 0, True)
+    iota(A("JD"), [[16, 16]], 3840, 0, True)
     fill(A("WT", 0, 256), 0.0)
     fill(A("EZ"), 0.0)
-    fill(A("FXE"), 0.0)
-    fill(A("FXO"), 0.0)
-    fill(A("ZRO"), 0.0)
-
-    def reset(n):
-        dmas([("y", A(n, 4096 + 2048 * c, 6144 + 2048 * c), A("ZRO")) for c in range(4)])
-
-    reset("SC0")
-    reset("SC1")
-    q1, kc, z0 = A("QI", 0, 1), A("KC", 0, 1), A("Z0", 0, 1)
     ts(A("KI", 0, 1), q1, 15, Op.bitwise_and)
     cp(kc, A("KI", 0, 1))
     ts(z0, kc, 0.5, Op.is_lt)
@@ -249,34 +234,29 @@ def rank_program(g, core, T, topo):
     ts(A("VF"), A("NV16"), 0.0625, Op.mult)
     for t in range(3):
         ts(A("KC%d" % t), A("ONE"), kc, Op.mult, 77.0 * t - 1280.0, Op.add)
-    cp(A("OCU"), A("OCP"))
-    ts(A("OE"), A("OCP"), 511.5, Op.is_lt)
-    ts(A("EE"), A("OCP"), 256.0, Op.add)
-    tt(A("O1"), A("EE"), A("OE"), Op.mult)
     cp(A("EZ", 15, 143, 16), A("BOF", 0, 128, 16))
-    ts(A("B1", 0, 1), q1, 1, Op.bitwise_and)
-    cp(A("ODD", 0, 1), A("B1", 0, 1))
-    ts(A("EVN", 0, 1), A("ODD", 0, 1), -1.0, Op.mult, 1.0, Op.add)
     ts(A("KB", 0, 1), kc, 1.5, Op.is_lt)
     act(A("IB"), A("IF"))
     act(A("EZ4"), A("EZ"), scale=4.0)
-    act(A("EZS"), A("EZ"), scale=kc)
     fill(A("CADD"), float(7 - rank))
-
-    npl = A("NPL")
+    ts(A("OE"), A("OCP"), 511.5, Op.is_lt)
+    ts(A("EE"), A("OCP"), 256.0, Op.add)
+    tt(A("O"), A("EE"), A("OE"), Op.mult)
 
     def ez(n, k):
         return A(n, 15 - k, 143 - k)
 
-    def lists(t, o16):
-        mms(A("P2", 0, 256), [(A("SH2"), o16), (A("I16"), A("C1"))])
-        kct = A("KC%d" % t)
-        mms(A("P3", 0, 256), [(A("I37"), o16), (A("IX16"), A("VF")), (A("I16"), kct)])
+    def persons():
+        cp(A("O16"), A("O"))
+        cp(A("OU"), A("O"))
+
+    def lists(t):
+        mms(A("P2", 0, 256), [(A("SH2"), A("O16")), (A("I16"), A("C1"))])
+        mms(A("P3", 0, 256), [(A("I37"), A("O16")), (A("IX16"), A("VF")), (A("I16"), A("KC%d" % t))])
         for b in range(2):
-            o = A("P3", 256 + 128 * b, 384 + 128 * b)
-            mms(o, [(A("I37"), A("O16", 128 * b, 128 * b + 128)), (A("IX16"), A("VF", 128 - 128 * b, 256 - 128 * b)),
-                    (A("I16"), A("KC%d" % t, 0, 128))])
-        tt(A("T1"), npl, A("P2", 0, 256), Op.mult)
+            mms(A("P3", 256 + 128 * b, 384 + 128 * b),
+                [(A("I37"), A("O16", 128 * b, 128 * b + 128)), (A("IX16"), A("VF", 128 - 128 * b, 256 - 128 * b)), (A("I16"), A("KC%d" % t, 0, 128))])
+        tt(A("T1"), A("NPL"), A("P2", 0, 256), Op.mult)
         ts(A("TQ"), A("T1"), 4, Op.arith_shift_right)
         tt(A("H", 0, 256), A("TQ"), A("P3", 0, 256), Op.add)
         ts(A("HA", 0, 256), A("H", 0, 256), 4095, Op.bitwise_and)
@@ -285,12 +265,6 @@ def rank_program(g, core, T, topo):
             tt(A("H", 256 + 128 * b, 384 + 128 * b), A("TQ", 128 - 128 * b, 256 - 128 * b), A("P3", 256 + 128 * b, 384 + 128 * b), Op.add)
         ts(A("HA", 256, 512), A("H", 256, 512), 4095, Op.bitwise_and)
         cp(A("HU", 256, 512), A("HA", 256, 512))
-
-    def persons(first):
-        if not first:
-            ts(A("O1"), A("ZI"), 4, Op.arith_shift_right)
-        cp(A("O16"), A("O1"))
-        cp(A("OU"), A("O1"))
 
     def wants():
         for c in (0, 2, 1, 3):
@@ -306,35 +280,20 @@ def rank_program(g, core, T, topo):
             mm(o, A("IB"), A("CADD"), True, False)
             mms(o, [(ez("EZ4", k), A(n, 1024 * c + k, 1024 * c + 1024 - 15 + k, 16)) for k in range(16)], False, True)
 
-    def slots_gather():
-        for c in (0, 2, 1, 3):
-            tt(A("MG", 1024 * c, 1024 * c + 1024), IND(A("QW"), A("OCU", 64 * c, 64 * c + 64)), A("NWI", 1024 * c, 1024 * c + 1024), Op.is_equal)
-            mms(A("P4", 64 * c, 64 * c + 64), [(ez("EZS", k), A("MG", 1024 * c + k, 1024 * c + 1024 - 15 + k, 16)) for k in range(16)])
-
-    persons(True)
-    lists(0, A("O16"))
+    for c in range(2):
+        act(A("WDS", 2048 * c, 2048 * c + 2048), A("ZRO"))
+    dmas([("y", A("WDE", 2048 * c, 2048 * c + 2048), A("ZRO")) for c in range(2)])
+    persons()
+    lists(0)
     wants()
 
-    def slots_of_places():
-        ts(A("EE"), A("OCP"), 16.0, Op.mult, 4096.0, Op.add)
-        tt(A("MC"), A("EE"), A("P4", 0, 256), Op.add)
-        tt(A("DD"), A("MC"), A("OE"), Op.mult)
-        tt(A("Z"), A("DD"), npl, Op.max)
-        cp(A("ZI"), A("Z"))
-
-    for n, x, y in (("FXE", "PA", "PB"), ("FXO", "PB", "PA")):
-        cp(A(n, 0, 1024, 16), A(x))
-        cp(A(n, 1, 1024, 16), A(y))
-    act(A("FN"), A("FXE", 0, 128), scale=-1.0)
-    act(A("PXE"), A("IF"), scale=A("EVN", 0, 1))
-    act(A("PXO"), A("IF"), scale=A("ODD", 0, 1))
-    act(A("PSE"), A("TA"), scale=A("EVN", 0, 1))
-    act(A("PSO"), A("TC"), scale=A("ODD", 0, 1))
     act(A("BO"), A("BOF"))
+    act(A("BOP"), A("BOF"), scale=A("KB", 0, 1))
     act(A("TRI"), A("TD"))
+    act(A("TRQ"), A("TD"), scale=-128.0)
+    act(A("TRN"), A("TD"), scale=-1.0)
     act(A("IBIG"), A("IF"), scale=-33554432.0)
-    act(A("NHI"), A("NV16"), bias=-4096.0)
-    act(A("NLO"), A("ONE"), scale=kc)
+    act(A("I8K"), A("IF"), scale=8192.0)
     for c in range(3):
         w0, w1 = 2048 * c, min(4336, 2048 * c + 2048)
         act(A("AH", w0, w1), A("ZRO", 0, w1 - w0))
@@ -344,10 +303,29 @@ def rank_program(g, core, T, topo):
         act(A("HM%d" % t), A("ZRO", 0, 256))
     act(A("MV", 256, 272), A("ZRO", 0, 16))
     act(A("T2", 512, 528), A("ZRO", 0, 16))
+    act(A("WDS", 4096, 4112), A("ZRO", 0, 16))
+    ts(A("Z4K", 0, 1), z0, 4096.0, Op.mult)
+    act(A("WDE", 4096, 4112), A("ONE", 0, 16), scale=A("Z4K", 0, 1))
+    act(A("NLQ"), A("ZRO", 0, 128))
+    act(A("NLN"), A("ZRO", 0, 128))
     ts(A("RS"), A("BOF", 0, 128, 16), A("KB", 0, 1), Op.mult)
     fill(A("RMN"), -1.0e6)
     fill(A("RMN", 0, 512, 16), 1.0e6)
     act(A("RMX"), A("RMN"), scale=-1.0)
+
+    def slot_windows():
+        q = A("QW")
+        ts(A("W1"), q, 0x1800, Op.bitwise_and)
+        ts(A("W2"), q, 5, Op.arith_shift_right, 0x38, Op.bitwise_and)
+        ts(A("W3"), q, 4, Op.arith_shift_right, 7, Op.bitwise_and)
+        ts(A("W5"), q, 1, Op.arith_shift_right, 0x40, Op.bitwise_and)
+        tt(A("W6"), A("W1"), A("W2"), Op.add)
+        ts(A("H"), q, 128.0, Op.mult)
+        tt(A("W7"), A("W3"), A("W5"), Op.add)
+        ts(A("HA"), A("H"), 0x780, Op.bitwise_and)
+        tt(A("W8"), A("W6"), A("W7"), Op.add)
+        tt(A("W9"), A("W8"), A("HA"), Op.add)
+        cp(A("WL"), A("W9"))
 
     def late_constants():
         ts(A("RW"), A("BOF", 0, 128, 16), kc, Op.mult, 16.0, Op.mult)
@@ -357,15 +335,16 @@ def rank_program(g, core, T, topo):
         act(A("TA"), one, scale=A("LIM", 0, 1))
         for c in range(4):
             mm(A("P5", 8 * c, 8 * c + 8), A("WT", 256 + 128 * c, 384 + 128 * c), A("RW"))
-        mm(A("P6", 0, 8), A("TA"), A("G0"))
+        mm(A("P4", 0, 8), A("TA"), A("G0"))
         for t in range(3):
             ts(A("HM%d" % t, t, 256, 8), A("ONE", 0, 32), z0, Op.mult, -1.0e6, Op.mult)
         ts(A("WSI"), A("P5", 0, 32), 255.0, Op.add)
         for c in range(4):
-            cp(A("L4P", 8 * c, 8 * c + 8), A("P6", 0, 8))
+            cp(A("L4P", 8 * c, 8 * c + 8), A("P4", 0, 8))
         ts(A("WSJ"), A("WSI"), 255, Op.bitwise_and)
         ts(A("W4"), A("WSJ"), 4.0, Op.mult, 32768.0, Op.add)
         ts(A("KC16", 0, 1), kc, -1.0, Op.mult, 16.0, Op.add)
+        ts(A("Z1", 0, 1), kc, 1.0, Op.is_equal)
         fill(A("MT", 0, 256), 131072.0)
         fill(A("R01"), 1.0)
         fill(A("R01", 0, 512, 16), 0.0)
@@ -384,64 +363,61 @@ def rank_program(g, core, T, topo):
         ts(A("PHF", 0, 1), A("PG", 0, 1), -1.0, Op.mult, 1.0, Op.add)
         ts(A("JW0", 0, 1), w, A("PHF", 0, 1), Op.mult, 2.0 ** -63, Op.mult)
         ts(A("PI", 7, 8), q1, 4, Op.arith_shift_right)
-        ts(A("PHF", 1, 2), A("PI", 7, 8), 256.0, Op.mult)
+        ts(A("PHF", 1, 2), A("PI", 7, 8), 16.0, Op.mult)
         for c in range(4):
-            ts(A("TT2", 128 * c, 128 * c + 128, 16), A("ONE", 0, 8), A("PHF", 1, 2), Op.mult, 4096.0 + 2048.0 * c, Op.add)
-        ts(A("TT2", 1, 512, 16), A("ONE", 0, 32), kc, Op.mult, 16.0, Op.mult)
-        for j in range(4):
-            fill(A("BC", j, j + 1), -2.0 * (2.0 ** (23 - 3 * j)) ** 2)
+            ts(A("TT2", 128 * c, 128 * c + 128, 16), A("ONE", 0, 8), A("PHF", 1, 2), Op.mult, 256.0 + 128.0 * c, Op.add)
+        ts(A("TT2", 1, 512, 16), A("ONE", 0, 32), kc, Op.mult)
+        ts(A("KW", 0, 1), kc, 2.0, Op.is_equal)
+        ts(A("KW", 1, 2), A("KB", 0, 1), 16.0, Op.mult)
+        tt(A("KW", 2, 3), A("KW", 0, 1), A("KW", 1, 2), Op.add)
+        act(A("EZW"), A("EZ"), scale=A("KW", 2, 3))
+        ts(A("JC"), A("JD"), kc, Op.add)
         fill(A("BC", 4, 5), -2000.0 * 63.2 * LN2)
+        act(A("NLQ", 0, 128, 16), A("BOF", 0, 128, 16), scale=-128.0)
+        act(A("NLN", 1, 128, 16), A("BOF", 0, 128, 16), scale=-1.0)
+        ts(A("NQ"), A("ONE"), kc, Op.mult, 128.0, Op.mult)
+        tt(A("NQ"), A("NQ"), A("WV"), Op.add)
+        ts(A("HV"), A("WV"), 2047.5, Op.is_gt, 2048.0, Op.mult)
+        tt(A("E1"), A("WV"), A("HV"), Op.subtract)
+        ts(A("E2"), A("E1"), A("Z1", 0, 1), Op.mult)
+        ts(A("E3"), A("HV"), 2048.0, Op.add, z0, Op.mult)
+        tt(A("CQ"), A("E2"), A("E3"), Op.add)
+        ts(A("E2"), A("NV16"), z0, Op.mult)
+        ts(A("E3"), A("ONE"), A("Z1", 0, 1), Op.mult, 16.0, Op.mult)
+        tt(A("CN"), A("E2"), A("E3"), Op.add)
+        for x in range(16):
+            mm(A("P4", x, 256 - 15 + x, 16), A("IB"), A("CQ", 16 * x, 16 * x + 16))
+        for x in range(16):
+            mm(A("P5", x, 256 - 15 + x, 16), A("IB"), A("CN", 16 * x, 16 * x + 16))
+        act(A("ATQ"), A("P4", 0, 256))
+        act(A("ATN"), A("P5", 0, 256))
 
     def pair_limits():
-        ts(A("ZU"), A("Z"), 0.0, Op.add)
-        tt(A("MN"), A("Z", 0, 128), A("Z", 128, 256), Op.min)
-        ts(A("TR"), A("MN"), 4095.5, Op.is_lt, 1.0e6, Op.mult)
+        tt(A("MN"), A("O", 0, 128), A("O", 128, 256), Op.min)
+        ts(A("TR"), A("MN"), 255.5, Op.is_lt, 1.0e6, Op.mult)
 
-    def decide(hv):
+    def decide(hv, heads):
         p = "P%d" % hv
-        m, d = A("MC", 128 * hv, 128 * hv + 128), A("DD", 128 * hv, 128 * hv + 128)
-        act(m, A(p, 0, 128))
+        w = (128 * hv, 128 * hv + 128)
+        m, d = A("MC", *w), A("DD", *w)
+        cp(m, A(p, 0, 128))
         tt(d, A(p, 128, 256), m, Op.subtract)
         pr, tr = A("PR", 64 * hv, 64 * hv + 64), A("TR", 64 * hv, 64 * hv + 64)
-        tt(pr, A("DD", 128 * hv, 128 * hv + 64), A("DD", 128 * hv + 64, 128 * hv + 128), Op.add)
+        tt(pr, A("DD", w[0], w[0] + 64), A("DD", w[0] + 64, w[1]), Op.add)
         for b in range(2):
-            tt(A("SWD", 128 * hv + 64 * b, 128 * hv + 64 * b + 64), pr, tr, Op.is_gt)
-        tt(A("EE", 128 * hv, 128 * hv + 128), d, A("SWD", 128 * hv, 128 * hv + 128), Op.mult)
-        f = A("F", 128 * hv, 128 * hv + 128)
-        tt(f, A("EE", 128 * hv, 128 * hv + 128), m, Op.add)
-        hi, lo = A("FHI", 128 * hv, 128 * hv + 128), A("FLO", 128 * hv, 128 * hv + 128)
-        act(hi, f)
+            tt(A("SWD", w[0] + 64 * b, w[0] + 64 * b + 64), pr, tr, Op.is_gt)
+        tt(A("EE", *w), d, A("SWD", *w), Op.mult)
+        f = A("F", *w)
+        tt(f, A("EE", *w), m, Op.add)
+        hi, lo = A("FHI", *w), A("FLO", *w)
+        cp(hi, f)
         tt(lo, f, hi, Op.subtract)
-        spread(hv, hi, lo)
+        dmas([("y", ROW("WDS", 0, 2048 * hv, 2048 * hv + 2048), hi), ("y", ROW("WDS", 1, 2048 * hv, 2048 * hv + 2048), lo)])
+        h = A("WDS", 2048 * hv + heads, 2048 * hv + 128, 8)
+        act(h, h, scale=-1.0)
 
-    def spread(hv, hi, lo):
-        p = "P%d" % (2 + hv)
-        mms(A(p, 0, 128), [(A("PXE"), hi), (A("PSE"), lo)])
-        mms(A(p, 128, 256), [(A("PXO"), hi), (A("PSO"), lo)])
-        act(A("XX", 256 * hv, 256 * hv + 256), A(p, 0, 256))
-
-    ebank = [0]
-
-    def widen(hv, b3, h, dst, heads):
-        p = "P%d" % (4 + ebank[0] % 3)
-        ebank[0] += 1
-        for k in range(16):
-            f = A("FXO" if k & 1 else "FXE", 128 * (k >> 1), 128 * (k >> 1) + 128)
-            x0 = 256 * hv + 128 * (k & 1) + 64 * b3 + 32 * h
-            mm(A(p, k, 512 - 15 + k, 16), f, A("XX", x0, x0 + 32))
-        if heads is not None:
-            x0 = 256 * hv + 64 * b3 + 32 * h
-            mm(A(p, 16 * heads, 512, 128), A("FN"), A("XX", x0 + heads, x0 + 32, 8))
-        j = 1024 * (2 * b3 + hv) + 512 * h
-        act(A(dst, j, j + 512), A(p))
-
-    def put(hv, b3, h, sc, src):
-        c0 = 64 * (2 * b3 + hv) + 32 * h
-        scatter(A(sc), A("ZU", c0, c0 + 32), A(src, 16 * c0, 16 * c0 + 512))
-
-    peers = [d for d in T.cores if d != core]
     used, plan = [], []
-    for d in sorted(peers, key=lambda d: len(topo.engines(core, d))):
+    for d in sorted([d for d in T.cores if d != core], key=lambda d: len(topo.engines(core, d))):
         es = [e for e in topo.engines(core, d) if e not in used][:4]
         used += es
         plan.append((d, sum(1 << e for e in es), len(es)))
@@ -454,8 +430,8 @@ def rank_program(g, core, T, topo):
             rid, pid = topo.addr(d, core)
             tr.append(RemoteDMATransfer(dst_ids=[DstId(rid=rid, pnc=pid)], dma_engine_mask=mask, remote_sem=T.sem["arr%d" % t], src=own, dst=own))
         g.remote_dma_fused(tr, local_sem=T.sem.sent)
-        cnt["sent"] = cnt.get("sent", 0) + sum(p[2] for p in plan)
         n = sum([p[2] for p in plan])
+        cnt["sent"] = cnt.get("sent", 0) + n
         tok = ("arr%d" % t, n)
         cnt[tok[0]] = n
         snap[tok] = {tok[0]: n}
@@ -463,16 +439,26 @@ def rank_program(g, core, T, topo):
             if r != rank:
                 hist.setdefault("LAND%d" % t, []).append(((32 * r, 32 * r + 32, 1), tok, "net", True, True))
 
-    def roll(t, sc):
+    def slot_scores():
         for c in range(4):
+            for m in (2 * c, 2 * c + 1):
+                o, i = A("GS", 1024 * m, 1024 * m + 1024), IND(A("WDS"), A("WL", 64 * m, 64 * m + 64))
+                if m & 1:
+                    cp(o, i)
+                else:
+                    act(o, i)
+            p = "P7" if c & 2 else "P6"
             for s in range(16):
-                lo = 4096 + 2048 * c + s
-                mm(A("P7", 128 * c + s, 128 * c + 128 - 15 + s, 16), A(sc, lo, lo + 2048 - 15, 16), A("RS"))
-        scan(A("PMN"), A("RMN"), A("P7"), 0.0, Op.max, Op.min)
-        scan(A("SMX"), A("RMX"), A("P7"), 0.0, Op.min, Op.max)
+                lo = 2048 * c + s
+                mm(A(p, 128 * (c & 1) + s, 128 * (c & 1) + 128 - 15 + s, 16), A("GS", lo, lo + 2048 - 15, 16), A("RS"))
+        for h, p in ((0, "P6"), (1, "P7")):
+            w = (256 * h, 256 * h + 256)
+            scan(A("PMN", *w), A("RMN", 0, 256), A(p, 0, 256), 0.0, Op.max, Op.min)
+            scan(A("SMX", *w), A("RMX", 0, 256), A(p, 0, 256), 0.0, Op.min, Op.max)
+
+    def roll(t):
         ts(A("YN"), A("PMN", 15, 512, 16), -1.0, Op.mult)
-        key = A("LAND%d" % t, 32 * rank, 32 * rank + 32)
-        tt(key, A("YN"), A("SMX", 15, 512, 16), Op.max)
+        tt(A("LAND%d" % t, 32 * rank, 32 * rank + 32), A("YN"), A("SMX", 15, 512, 16), Op.max)
         send(t)
 
     def after_exchange(t):
@@ -480,19 +466,24 @@ def rank_program(g, core, T, topo):
         for hv in range(2):
             cp(A("SW", 64 * hv, 64 * hv + 64), A("SWD", 128 * hv, 128 * hv + 64))
             tt(A("DF", 64 * hv, 64 * hv + 64), A("F", 128 * hv, 128 * hv + 64), A("F", 128 * hv + 64, 128 * hv + 128), Op.subtract)
-        tt(A("DZ"), A("Z", 0, 128), A("Z", 128, 256), Op.subtract)
+        tt(A("DZ"), A("O", 0, 128), A("O", 128, 256), Op.subtract)
         tt(A("ZS"), A("DZ"), A("SW"), Op.mult)
         tt(A("FS"), A("DF"), A("SW"), Op.mult)
-        tt(A("Z2", 0, 128), A("Z", 0, 128), A("ZS"), Op.subtract)
-        tt(A("Z2", 128, 256), A("Z", 128, 256), A("ZS"), Op.add)
-        cp(A("I2"), A("Z2"))
-        ts(A("O2"), A("I2"), 4, Op.arith_shift_right)
-        cp(A("OU2"), A("O2"))
+        tt(A("O2H", 0, 128), A("O", 0, 128), A("ZS"), Op.subtract)
+        tt(A("O2H", 128, 256), A("O", 128, 256), A("ZS"), Op.add)
+        cp(A("OU2"), A("O2H"))
         for hv in range(2):
             tt(A("F2", 64 * hv, 64 * hv + 64), A("F", 128 * hv, 128 * hv + 64), A("FS", 64 * hv, 64 * hv + 64), Op.subtract)
             tt(A("F2", 128 + 64 * hv, 192 + 64 * hv), A("F", 128 * hv + 64, 128 * hv + 128), A("FS", 64 * hv, 64 * hv + 64), Op.add)
         tt(A("FL"), A("F2"), A("HBL"), Op.add)
         ts(A("MYK"), A("LAND%d" % t, 32 * rank, 32 * rank + 32), 0.5, Op.max)
+
+    def place_keys(c, vec):
+        o, i = A("MG", 1024 * c, 1024 * c + 1024), IND(A("MT"), A("OU2", 64 * c, 64 * c + 64))
+        if vec:
+            cp(o, i)
+        else:
+            act(o, i)
 
     def thresholds(t):
         ld = "LAND%d" % t
@@ -503,9 +494,8 @@ def rank_program(g, core, T, topo):
         for c in range(4):
             mm(A("P0", 128 * c, 128 * c + 128), A("TT0", 128 * c, 128 * c + 128), A("IB"))
         act(A("MT", 256, 768), A("P0"))
-        for c in range(4):
-            act(A("MG", 1024 * c, 1024 * c + 1024), IND(A("MT"), A("OU2", 64 * c, 64 * c + 64)))
-            mms(A("P1", 64 * c, 64 * c + 64), [(ez("EZ", k), A("MG", 1024 * c + k, 1024 * c + 1024 - 15 + k, 16)) for k in range(16)])
+        for c in range(3):
+            place_keys(c, False)
 
     def applicants():
         tt(A("KD"), A("K"), A("L4P"), Op.subtract)
@@ -519,9 +509,10 @@ def rank_program(g, core, T, topo):
         tt(A("TM"), A("TU"), A("AP"), Op.mult)
         ts(A("UH"), A("TM"), 2, Op.arith_shift_right, 0x20E8, Op.bitwise_and)
         ts(A("UL"), A("TM"), 2, Op.arith_shift_right, 0x17, Op.bitwise_and)
-        ts(A("TT2", 2, 512, 16), A("P3", 0, 32), 0.0, Op.add)
+        cp(A("TT2", 2, 512, 16), A("P3", 0, 32))
         for c in range(4):
             mm(A("P7", 128 * c, 128 * c + 128), A("TT2", 128 * c, 128 * c + 128), A("IB"))
+        place_keys(3, True)
         for x in range(16):
             v = 0x2000 + 8 * (x >> 3 & 1) + 128 * (x >> 2 & 1) + 64 * (x >> 1 & 1) + 32 * (x & 1)
             ts(A("AH", 112 + x, 112 + x + 128 * 31 + 1, 128), A("UH"), float(v), Op.is_equal)
@@ -531,129 +522,146 @@ def rank_program(g, core, T, topo):
         for j in range(2):
             ts(A("BL", 512 * j, 512 * j + 512), A("B0L"), A("JW%d" % j, 0, 1), Op.mult)
         for c in range(4):
+            mms(A("P1", 64 * c, 64 * c + 64), [(ez("EZ", k), A("MG", 1024 * c + k, 1024 * c + 1024 - 15 + k, 16)) for k in range(16)])
+        act(A("T2", 0, 512), A("P7"))
+
+    def leave(t):
+        tt(A("LV"), A("FL"), A("P1", 0, 256), Op.is_lt)
+        mms(A("P3", 0, 256), [(A("TRN" if t == 2 else "TRQ"), A("LV")), (A("I8K"), A("LV"))])
+        for h in range(2):
+            mm(A("P5", 128 * h, 128 * h + 128), A("LV", 128 * h, 128 * h + 128), A("TRI"))
+        for h in range(2):
+            mms(A("P4", 128 * h, 128 * h + 128), [(A("O2H", 128 * h, 128 * h + 128), A("I16")), (A("LV", 128 * h, 128 * h + 128), A("IBIG"))])
+        mm(A("P2", 0, 256), A("BO"), A("LV"))
+        for x in range(16):
+            mm(A("P2", 256 + x, 512 - 15 + x, 16), A("NLN" if t == 2 else "NLQ"), A("LV", 16 * x, 16 * x + 16))
+        for x in range(16):
+            mm(A("P7", 0, 16), ez("EZ", x), A("LV", 16 * x, 16 * x + 16), x == 0, x == 15)
+        tt(A("E1"), A("NPL" if t == 2 else "NQ"), A("P3", 0, 256), Op.add)
+        ts(A("BT"), A("P5", 0, 256), float(2 ** 23 + 2 ** 19 + 2 ** 15 + 2 ** 11), Op.mult)
+        tt(A("DE"), A("E1", 0, 128), A("E1", 128, 256), Op.subtract)
+        ts(A("BT2"), A("BT"), 2 ** 23 + 2 ** 20 + 2 ** 17 + 2 ** 14, Op.bitwise_and)
+        tt(A("ES"), A("DE"), A("SW"), Op.mult)
+        tt(A("Y"), A("BT2"), A("P4", 0, 256), Op.add)
+        for hv in range(2):
+            es = A("ES", 64 * hv, 64 * hv + 64)
+            tt(A("E2", 128 * hv, 128 * hv + 64), A("E1", 64 * hv, 64 * hv + 64), es, Op.subtract)
+            tt(A("E2", 128 * hv + 64, 128 * hv + 128), A("E1", 128 + 64 * hv, 192 + 64 * hv), es, Op.add)
+        ts(A("E3"), A("E2"), 4096.0, Op.min)
+        act(A("EHI"), A("E3"))
+        tt(A("ELO"), A("E3"), A("EHI"), Op.subtract)
+        dmas([("y", ROW("WDE", i, 2048 * hv, 2048 * hv + 2048), A(n, 128 * hv, 128 * hv + 128)) for hv in range(2) for i, n in ((0, "EHI"), (1, "ELO"))])
+
+    def move_slots(chunks, both=False):
+        for m in chunks:
+            o, i = A("GE", 256 + 1024 * m, 1280 + 1024 * m), IND(A("WDE"), A("WL", 64 * m, 64 * m + 64))
+            if both and m & 1:
+                cp(o, i)
+            else:
+                act(o, i)
+
+    def join_slots():
+        scatter(A("GE"), A("SU"), A("AT"))
+
+    def read_slots(h):
+        mms(A("P5", 256 * h, 256 * h + 256), [(ez("EZ", s), A("GE", 256 + 4096 * h + s, 256 + 4096 * h + 4096 - 15 + s, 16)) for s in range(16)])
+
+    def close_up(j):
+        th, d = 2.0 ** (23 - 3 * j), 1 << j
+        ts(A("P5", 0, 256), A("Y"), th, Op.is_lt)
+        ts(A("MV", 0, 256), A("Y"), th, Op.subtract, 0.0, Op.max)
+        tt(A("P5", 256, 512), A("Y"), A("P5", 0, 256), Op.mult)
+        tt(A("Y"), A("P5", 256, 512), A("MV", d, 256 + d), Op.max)
+
+    def logs():
+        for c in range(4):
             for h in range(8):
                 cg = 8 * c + h
                 w0 = 112 + 128 * cg - 16 * h
                 mm(A("P6", c, 128 - 3 + c, 4), A("AH", w0, w0 + 128), A("BL", cg, 1024 - 31 + cg, 32), h == 0, h == 7)
-        act(A("T2", 0, 512), A("P7"))
         act(A("LT"), A("P6", 0, 128), Act.Ln, bias=2.0 ** -64)
         act(A("PEN"), A("LT"), Act.Relu, bias=A("BC", 4, 5), scale=-2000.0)
 
-    def winners():
+    def winners(t):
         tt(A("K1"), A("CK"), A("LT"), Op.subtract)
         tt(A("K2"), A("K1"), A("PEN"), Op.add)
         scan(A("KM"), A("RK"), A("K2"), 0.0, Op.max, Op.min)
         tt(A("PM"), A("KM", 3, 64, 4), A("KM", 67, 128, 4), Op.min)
+        ts(A("PF"), A("P7", 0, 16), 0.5, Op.is_lt, 1.0e4, Op.mult)
+        tt(A("PM"), A("PM"), A("PF"), Op.max)
         ts(A("PMI"), A("PM"), 0.5 / LN2, Op.mult, 512.0, Op.min)
         cp(A("PU"), A("PMI"))
         act(A("G2"), IND(A("T2"), A("PU")))
         for x in range(16):
-            mm(A("P3", 256 + 16 * x, 272 + 16 * x), A("BO"), A("G2", x, 256 - 15 + x, 16))
+            mm(A("P6", 16 * x, 16 * x + 16), A("BOP"), A("G2", x, 256 - 15 + x, 16))
+        for x in range(16):
+            mm(A("P6", 256, 272), ez("EZW", x), A("G2", x, 256 - 15 + x, 16), x == 0, x == 15)
 
-    def leave():
-        tt(A("LV"), A("FL"), A("P1", 0, 256), Op.is_lt)
+    def settle(t):
         for h in range(2):
-            z = A("P4", 256 + 128 * h, 384 + 128 * h)
-            lv = A("LV", 128 * h, 128 * h + 128)
-            mm(A("P4", 128 * h, 128 * h + 128), lv, A("TRI"))
-            mm(z, A("Z2", 128 * h, 128 * h + 128), A("IF"), True, False)
-            mm(z, lv, A("IBIG"), False, True)
-        mm(A("P2", 0, 256), A("BO"), A("LV"))
-        ts(A("BT"), A("P4", 0, 256), float(2 ** 23 + 2 ** 19 + 2 ** 15 + 2 ** 11), Op.mult)
-        ts(A("BT2"), A("BT"), 2 ** 23 + 2 ** 20 + 2 ** 17 + 2 ** 14, Op.bitwise_and)
-        tt(A("Y"), A("BT2"), A("P4", 256, 512), Op.add)
-
-    def close_up(j):
-        th, d = 2.0 ** (23 - 3 * j), 1 << j
-        act(A("P5", 0, 256), A("Y"), Act.Relu, bias=A("BC", j, j + 1), scale=2.0 * th)
-        ts(A("MV", 0, 256), A("Y"), th, Op.subtract, 0.0, Op.max)
-        tt(A("P5", 256, 512), A("Y"), A("P5", 0, 256), Op.subtract)
-        tt(A("Y"), A("P5", 256, 512), A("MV", d, 256 + d), Op.max)
-
-    def settle(last):
-        for h in range(2):
-            mm(A("P0", 128 * h, 128 * h + 128), A("Y", 128 * h, 128 * h + 128), A("IF"))
+            mm(A("P1", 128 * h, 128 * h + 128), A("Y", 128 * h, 128 * h + 128), A("IF"))
         ts(A("EQ"), A("P2", 0, 256), A("KC16", 0, 1), Op.is_equal)
-        tt(A("AC"), A("EQ"), A("P3", 256, 512), Op.mult)
-        tt(A("APP"), A("AC"), npl, Op.max)
-        tt(A("ZI"), A("P0", 0, 256), A("APP"), Op.max)
-
-    def place_numbers():
-        for hv in range(2):
-            p = "P%d" % (2 + hv)
-            for n, (e, f) in ((0, ("PXE", "PSE")), (128, ("PXO", "PSO"))):
-                for b in range(2):
-                    x0 = 128 * b + 64 * hv
-                    mms(A(p, n + 64 * b, n + 64 * b + 64), [(A(e), A("NHI", x0, x0 + 64)), (A(f), A("NLO", x0, x0 + 64))])
-            act(A("XX", 256 * hv, 256 * hv + 256), A(p, 0, 256))
-            for b3 in range(2):
-                for h in range(2):
-                    widen(hv, b3, h, "WN", None)
+        tt(A("AC"), A("EQ"), A("P6", 0, 256), Op.mult)
+        tt(A("O"), A("P1", 0, 256), A("AC"), Op.max)
+        if t < 2:
+            persons()
+        tt(A("JD"), A("P6", 256, 272), A("JC"), Op.max)
+        ts(A("SU"), A("JD"), -3840.0, Op.add)
+        tt(A("AT"), A("ATN" if t == 2 else "ATQ"), A("P2", 256, 512), Op.add)
 
     for t in range(3):
-        sc = "SC%d" % (t & 1)
         if t:
-            persons(False)
-            lists(t, A("O16"))
+            lists(t)
             wants()
+            move_slots(range(3, 8))
         minima(0)
         minima(2)
-        if t == 0:
-            slots_gather()
-            slots_of_places()
-        else:
-            cp(A("Z"), A("ZI"))
         pair_limits()
         minima(1)
-        decide(0)
+        decide(0, t)
+        if t:
+            join_slots()
+            read_slots(0)
         minima(3)
-        for b3 in range(2):
-            for h in range(2):
-                widen(0, b3, h, "WD", t)
-        put(0, 0, 0, sc, "WD")
-        put(0, 0, 1, sc, "WD")
-        decide(1)
-        for b3 in range(2):
-            for h in range(2):
-                widen(1, b3, h, "WD", t)
-        put(0, 1, 0, sc, "WD")
-        put(0, 1, 1, sc, "WD")
-        for b3 in range(2):
-            for h in range(2):
-                put(1, b3, h, sc, "WD")
-        if t == 1:
-            place_numbers()
-        roll(t, sc)
-        if t == 0:
+        if t:
+            read_slots(1)
+        else:
+            slot_windows()
+        decide(1, t)
+        if t:
+            cp(A("WL"), A("P5"))
+        else:
             late_constants()
+        slot_scores()
+        roll(t)
         after_exchange(t)
         thresholds(t)
-        if t:
-            reset("SC%d" % (t - 1 & 1))
         applicants()
-        leave()
+        leave(t)
+        logs()
         close_up(0)
-        winners()
-        for j in range(1, 4):
-            close_up(j)
-        settle(t == 2)
+        close_up(1)
+        winners(t)
+        close_up(2)
+        close_up(3)
+        settle(t)
+        if t < 2:
+            move_slots(range(3))
 
-    cp(A("ZU"), A("ZI"))
-    ts(A("O1"), A("ZI"), 4, Op.arith_shift_right)
-    for hv in range(2):
-        for b3 in range(2):
-            for h in range(2):
-                put(hv, b3, h, "SC1", "WN")
-    ts(A("OE"), A("O1"), 255.5, Op.is_lt, 768.0, Op.mult)
-    ts(A("EE"), A("O1"), -256.0, Op.add, 0.0, Op.max)
-    tt(A("AC"), A("EE"), A("OE"), Op.max)
-    ts(A("YO"), A("AC"), 512.0, Op.min)
+    move_slots(range(8), True)
+    join_slots()
+    ts(A("OE"), A("O"), 255.5, Op.is_lt, 512.0, Op.mult)
+    ts(A("EE"), A("O"), -256.0, Op.add)
+    tt(A("YO"), A("EE"), A("OE"), Op.max)
     dmas([("s", nat("YON", c), A("YO", 64 * c, 64 * c + 64)) for c in range(4)])
     dmas([("s", ext(T.yoc[:]), (T.YON[:], [("YON", 0, 1, 1)]))])
     for h in range(2):
-        p = "P%d" % h
-        mms(A(p, 0, 256), [(ez("EZ", s), A("SC1", 4096 + 4096 * h + s, 8192 + 4096 * h - 15 + s, 16)) for s in range(16)])
-        ts(A("YQ", 256 * h, 256 * h + 256), A(p, 0, 256), 4096.0, Op.add)
+        p = "P%d" % (4 + h)
+        mms(A(p, 0, 256), [(ez("EZ", s), A("GE", 256 + 4096 * h + s, 256 + 4096 * h + 4096 - 15 + s, 16)) for s in range(16)])
+        if h:
+            cp(A("YQ", 256, 512), A(p, 0, 256))
+        else:
+            act(A("YQ", 0, 256), A(p, 0, 256))
         dmas([("y", ext(T.yq[:, 256 * h:256 * h + 256]), A("YQ", 256 * h, 256 * h + 256))])
     for s in sorted(cnt):
         if known["g"].get(s, 0) < cnt[s]:

@@ -19,17 +19,17 @@ def _decl(dtype, spec):
     SCRATCH[pool] = ("sbuf", [128, at], dtype)
 
 
-_decl(BF, "XT:4096 WT:768 MT:768 T2:528 WG:4096 D0:4096 D1:4096 MG:4096 ZRO:2048 WDS:4112 WDE:4112 GS:8192 GE:8448 "
-          "EZ:144 EZ4:144 EZW:144 BO:128 BOP:128 IB:128 IBIG:128 I8K:128 TRI:128 TRQ:128 TRN:128 NLQ:128 NLN:128 "
+_decl(BF, "XT:4096 WT:768 MT:768 T2:528 WG:4096 D0:4096 D1:4096 MG:4096 ZRO:2112 WDS:4112 WDE:4112 GS:8448 GE:8448 "
+          "EZ:144 EZ4:144 EZM:144 EZW:144 INB:128 ULB:32 BO:128 BOP:128 IB:128 IBIG:128 I8K:128 TRI:128 TRQ:128 TRN:128 NLQ:128 NLN:128 "
           "RS:8 RW:8 CADD:64 FHI:256 FLO:256 EHI:256 ELO:256 CMP:512 TT0:512 TT2:512 AH:4336 B0L:512 BL:1024 G2:256 LV:256 AT:256 "
           "CQ:256 CN:256")
 _decl(FH, "SH2:128 I16:128 I37:128 IX16:128 C1:256 VF:256 KC0:256 KC1:256 KC2:256 O16:256 O2H:256")
-_decl(I4, "OCP:256 QW:512 THI:16 QI:8 KI:8 B1:8 PI:8 T1:256 TQ:256 H:512 HA:512 W1:512 W2:512 W3:512 W5:512 W6:512 W7:512 W8:512 W9:512 WSI:32 WSJ:32 TM:32 UH:32 UL:32 PMI:16 BT:256 BT2:256")
+_decl(I4, "OCP:256 QW:512 THI:16 QI:8 KI:8 B1:8 PI:8 T1:256 TQ:256 H:512 HA:512 W1:512 W2:512 W3:512 W6:512 W7:512 W9:512 WSI:32 WSJ:32 TM:32 UH:32 UL:32 PMI:16 BT:256 BT2:256")
 _decl(U2, "OU:256 HU:512 PU:16 SU:16 OU2:256 WL:512")
 _decl(F4, "IF:128 BOF:128 TA:128 TB:128 TC:128 TD:128 PA:64 PB:64 PG:8 JB:8 BC:8 G0:8 ONE:256 KC:8 KC16:8 KB:8 KW:8 Z0:8 Z1:8 Z4K:8 ODD:8 EVN:8 THF:8 LIM:8 "
           "JW0:8 JW1:8 JW:8 PHF:8 NV16:256 NPL:256 NQ:256 WV:256 HV:256 ATQ:256 ATN:256 JC:16 JD:16 C1F:256 HM0:256 HM1:256 HM2:256 HBL:256 "
           "O:256 OE:256 MN:128 TR:128 MC:256 DD:256 PR:128 SW:128 SWD:256 EE:256 E1:256 DE:128 ES:128 E2:256 E3:256 "
-          "F:256 SMX:512 PMN:512 RMX:512 RMN:512 R01:512 YN:32 MYK:32 KK:64 K:32 KD:32 KS:512 L4P:32 W4:32 HOLD:32 AP:32 TU:32 LT:128 PEN:128 CK:128 "
+          "F:256 YC:512 SMX:512 PMN:512 RMX:512 RMN:512 R01:512 YN:32 MYK:32 KK:64 K:32 KD:32 KS:512 L4P:32 W4:32 HOLD:32 AP:32 TU:32 LT:128 PEN:128 CK:128 "
           "RK:128 K1:128 K2:128 KM:128 PM:16 PF:16 DZ:128 ZS:128 DF:128 FS:128 F2:256 FL:256 Y:256 MV:272 EQ:256 AC:256 YO:256 YQ:512 "
           "LAND0:128 LAND1:128 LAND2:128")
 SCRATCH["OCN"] = ("sbuf", [128, 2, 8, 2, 8], I4)
@@ -38,7 +38,7 @@ for _i in range(8):
     SCRATCH["P%d" % _i] = ("psum", [128, 512], F4)
     WIDTH["P%d" % _i] = 512
     WHERE["P%d" % _i] = ("P%d" % _i, 0)
-SEMAPHORES = (["qv", "qs", "qt", "qg", "sent"] + ["arr%d" % t for t in range(3)] + ["d%d" % i for i in range(20)])
+SEMAPHORES = (["qv", "qs", "qt", "qg", "sent"] + ["arr%d" % t for t in range(3)] + ["d%d" % i for i in range(30)])
 
 
 def _bank(name):
@@ -208,6 +208,8 @@ def rank_program(g, core, T, topo):
         iota(A("NV16", 64 * c, 64 * c + 64), [[256, 8], [16, 8]], 2048 * (c & 1) + 128 * (c >> 1), 0, True)
     fill(A("ONE"), 1.0)
     fill(A("ZRO"), 0.0)
+    for c in range(2):
+        act(A("WDS", 2048 * c, 2048 * c + 2048), A("ZRO", 0, 2048))
     aff(A("IF"), one, [[-1, 128]], Op.is_equal, 0.0, 0, 1)
     aff(A("TA"), one, [[-1, 128]], Op.is_equal, 0.0, 1, 1)
     aff(A("TB"), one, [[-16, 8], [0, 16]], Op.is_ge, 0.0, 0, 1)
@@ -216,8 +218,9 @@ def rank_program(g, core, T, topo):
     aff(A("PG"), A("ONE", 0, 8), [[0, 8]], Op.is_ge, 0.0, -64, 1)
     iota(A("CK"), [[64, 2], [0, 16], [128, 4]], 0, 0, True)
     for c in range(4):
-        iota(A("WV", 64 * c, 64 * c + 64), [[1, 64]], 2048 * (c & 1) + 64 * (c >> 1), 0, True)
+        iota(A("WV", 64 * c, 64 * c + 64), [[1, 64]], 128 * (c & 1) + 64 * (c >> 1), 0, True)
     iota(A("JD"), [[16, 16]], 3840, 0, True)
+    iota(A("YC"), [[16, 2], [1, 8], [0, 32]], 0, 0, True)
     fill(A("WT", 0, 256), 0.0)
     fill(A("EZ"), 0.0)
     ts(A("KI", 0, 1), q1, 15, Op.bitwise_and)
@@ -232,13 +235,8 @@ def rank_program(g, core, T, topo):
     ts(A("C1F"), A("NV16"), 0.125, Op.mult, 512.0, Op.add)
     ts(A("C1"), A("C1F"), z0, Op.mult, -511.0, Op.add)
     ts(A("VF"), A("NV16"), 0.0625, Op.mult)
-    for t in range(3):
-        ts(A("KC%d" % t), A("ONE"), kc, Op.mult, 77.0 * t - 1280.0, Op.add)
-    cp(A("EZ", 15, 143, 16), A("BOF", 0, 128, 16))
-    ts(A("KB", 0, 1), kc, 1.5, Op.is_lt)
+    ts(A("KC0"), A("ONE"), kc, Op.mult, -1280.0, Op.add)
     act(A("IB"), A("IF"))
-    act(A("EZ4"), A("EZ"), scale=4.0)
-    fill(A("CADD"), float(7 - rank))
     ts(A("OE"), A("OCP"), 511.5, Op.is_lt)
     ts(A("EE"), A("OCP"), 256.0, Op.add)
     tt(A("O"), A("EE"), A("OE"), Op.mult)
@@ -266,6 +264,8 @@ def rank_program(g, core, T, topo):
         ts(A("HA", 256, 512), A("H", 256, 512), 4095, Op.bitwise_and)
         cp(A("HU", 256, 512), A("HA", 256, 512))
 
+    shared = [3]
+
     def wants():
         for c in (0, 2, 1, 3):
             act(A("WG", 1024 * c, 1024 * c + 1024), IND(A("WT"), A("OU", 64 * c, 64 * c + 64)))
@@ -273,24 +273,53 @@ def rank_program(g, core, T, topo):
     def minima(c):
         w = A("WG", 1024 * c, 1024 * c + 1024)
         for j, n in ((0, "D0"), (1, "D1")):
+            if j and c in shared:
+                continue
             tt(A(n, 1024 * c, 1024 * c + 1024), IND(A("XT"), A("HU", 256 * j + 64 * c, 256 * j + 64 * c + 64)), w, Op.min)
         hv, b3 = c & 1, c >> 1
         for j, n in ((0, "D0"), (1, "D1")):
             o = A("P%d" % hv, 128 * j + 64 * b3, 128 * j + 64 * b3 + 64)
             mm(o, A("IB"), A("CADD"), True, False)
-            mms(o, [(ez("EZ4", k), A(n, 1024 * c + k, 1024 * c + 1024 - 15 + k, 16)) for k in range(16)], False, True)
+            d = [A(n, 1024 * c + k, 1024 * c + 1024 - 15 + k, 16) for k in range(16)]
+            if j and c in shared:
+                mms(o, [(ez("EZ4", k), A("WG", 1024 * c + k, 1024 * c + 1024 - 15 + k, 16)) for k in range(16)], False, False)
+                mms(o, [(ez("EZM", k), d[k]) for k in range(16)], False, True)
+            else:
+                mms(o, [(ez("EZ4", k), d[k]) for k in range(16)], False, True)
 
-    for c in range(2):
-        act(A("WDS", 2048 * c, 2048 * c + 2048), A("ZRO"))
-    dmas([("y", A("WDE", 2048 * c, 2048 * c + 2048), A("ZRO")) for c in range(2)])
+    def shared_gather():
+        for c in shared:
+            act(A("D1", 1024 * c, 1024 * c + 1024), IND(A("XT"), A("HU", 256 + 64 * c, 320 + 64 * c)))
+
+    def shared_clip():
+        for c in shared:
+            for h in range(2):
+                w = (1024 * c + 512 * h, 1024 * c + 512 * h + 512)
+                mms(A("P%d" % (2 + h)), [(A("IB"), A("WG", *w)), (A("INB"), A("D1", *w))])
+                act(A("D1", *w), A("P%d" % (2 + h)), Act.Relu)
+
+    ts(A("PI", 0, 1), q1, 63, Op.bitwise_and)
+    cp(A("JB", 0, 1), A("PI", 0, 1))
+    fill(A("JB", 1, 2), 63.0 * LN2)
+    dmas([("y", A("WDE", 2048 * c, 2048 * c + 2048), A("ZRO", 0, 2048)) for c in range(2)])
     persons()
     lists(0)
+    cp(A("EZ", 15, 143, 16), A("BOF", 0, 128, 16))
+    fill(A("CADD"), float(7 - rank))
     wants()
+    act(A("EZ4"), A("EZ"), scale=4.0)
+    act(A("JW", 0, 1), A("JB", 0, 1), Act.Exp, bias=A("JB", 1, 2), scale=-2.0 * LN2)
+    act(A("EZM"), A("EZ"), scale=-4.0)
+    act(A("INB"), A("IF"), scale=-1.0)
+    shared_gather()
+    ts(A("KB", 0, 1), kc, 1.5, Op.is_lt)
+    for t in (1, 2):
+        ts(A("KC%d" % t), A("ONE"), kc, Op.mult, 77.0 * t - 1280.0, Op.add)
 
     act(A("BO"), A("BOF"))
     act(A("BOP"), A("BOF"), scale=A("KB", 0, 1))
     act(A("TRI"), A("TD"))
-    act(A("TRQ"), A("TD"), scale=-128.0)
+    act(A("TRQ"), A("TD"), scale=-256.0)
     act(A("TRN"), A("TD"), scale=-1.0)
     act(A("IBIG"), A("IF"), scale=-33554432.0)
     act(A("I8K"), A("IF"), scale=8192.0)
@@ -315,17 +344,15 @@ def rank_program(g, core, T, topo):
 
     def slot_windows():
         q = A("QW")
-        ts(A("W1"), q, 0x1800, Op.bitwise_and)
+        ts(A("H"), q, 256.0, Op.mult)
+        ts(A("W1"), q, 4, Op.arith_shift_right, 0x87, Op.bitwise_and)
         ts(A("W2"), q, 5, Op.arith_shift_right, 0x38, Op.bitwise_and)
-        ts(A("W3"), q, 4, Op.arith_shift_right, 7, Op.bitwise_and)
-        ts(A("W5"), q, 1, Op.arith_shift_right, 0x40, Op.bitwise_and)
+        ts(A("W3"), q, 1, Op.arith_shift_right, 0x40, Op.bitwise_and)
+        ts(A("HA"), A("H"), 0x100F00, Op.bitwise_and)
         tt(A("W6"), A("W1"), A("W2"), Op.add)
-        ts(A("H"), q, 128.0, Op.mult)
-        tt(A("W7"), A("W3"), A("W5"), Op.add)
-        ts(A("HA"), A("H"), 0x780, Op.bitwise_and)
-        tt(A("W8"), A("W6"), A("W7"), Op.add)
-        tt(A("W9"), A("W8"), A("HA"), Op.add)
-        cp(A("WL"), A("W9"))
+        tt(A("W7"), A("W3"), A("HA"), Op.add)
+        tt(A("W9"), A("W6"), A("W7"), Op.add)
+        ts(A("WL"), A("W9"), 4096.0, Op.min)
 
     def late_constants():
         ts(A("RW"), A("BOF", 0, 128, 16), kc, Op.mult, 16.0, Op.mult)
@@ -351,17 +378,8 @@ def rank_program(g, core, T, topo):
         fill(A("RK"), -1.0e6)
         fill(A("RK", 0, 128, 4), 1.0e6)
         ts(A("CK"), A("CK"), 31.6, Op.add, 2.0 * LN2, Op.mult)
-        w = A("JW", 0, 1)
-        ts(A("B1", 1, 2), q1, -1.0, Op.mult, 127.0, Op.add)
-        for b in range(6):
-            f = A("JB", b, b + 1) if b else w
-            ts(A("PI", b, b + 1), A("B1", 1, 2), b, Op.arith_shift_right, 1, Op.bitwise_and)
-            ts(f, A("PI", b, b + 1), 4.0 ** (2 ** b) - 1.0, Op.mult, 1.0, Op.add)
-            if b:
-                tt(w, w, f, Op.mult)
-        ts(A("JW1", 0, 1), w, A("PG", 0, 1), Op.mult, 2.0 ** -63, Op.mult)
-        ts(A("PHF", 0, 1), A("PG", 0, 1), -1.0, Op.mult, 1.0, Op.add)
-        ts(A("JW0", 0, 1), w, A("PHF", 0, 1), Op.mult, 2.0 ** -63, Op.mult)
+        tt(A("JW1", 0, 1), A("JW", 0, 1), A("PG", 0, 1), Op.mult)
+        tt(A("JW0", 0, 1), A("JW", 0, 1), A("JW1", 0, 1), Op.subtract)
         ts(A("PI", 7, 8), q1, 4, Op.arith_shift_right)
         ts(A("PHF", 1, 2), A("PI", 7, 8), 16.0, Op.mult)
         for c in range(4):
@@ -373,16 +391,12 @@ def rank_program(g, core, T, topo):
         act(A("EZW"), A("EZ"), scale=A("KW", 2, 3))
         ts(A("JC"), A("JD"), kc, Op.add)
         fill(A("BC", 4, 5), -2000.0 * 63.2 * LN2)
-        act(A("NLQ", 0, 128, 16), A("BOF", 0, 128, 16), scale=-128.0)
+        act(A("NLQ", 0, 128, 16), A("BOF", 0, 128, 16), scale=-256.0)
         act(A("NLN", 1, 128, 16), A("BOF", 0, 128, 16), scale=-1.0)
-        ts(A("NQ"), A("ONE"), kc, Op.mult, 128.0, Op.mult)
+        ts(A("NQ"), A("ONE"), kc, Op.mult, 256.0, Op.mult)
         tt(A("NQ"), A("NQ"), A("WV"), Op.add)
-        ts(A("HV"), A("WV"), 2047.5, Op.is_gt, 2048.0, Op.mult)
-        tt(A("E1"), A("WV"), A("HV"), Op.subtract)
-        ts(A("E2"), A("E1"), A("Z1", 0, 1), Op.mult)
-        ts(A("E3"), A("HV"), 2048.0, Op.add, z0, Op.mult)
-        tt(A("CQ"), A("E2"), A("E3"), Op.add)
-        ts(A("E2"), A("NV16"), z0, Op.mult)
+        ts(A("CQ"), A("WV"), A("Z1", 0, 1), Op.mult)
+        ts(A("E2"), A("NV16"), -4096.0, Op.add, z0, Op.mult)
         ts(A("E3"), A("ONE"), A("Z1", 0, 1), Op.mult, 16.0, Op.mult)
         tt(A("CN"), A("E2"), A("E3"), Op.add)
         for x in range(16):
@@ -404,17 +418,20 @@ def rank_program(g, core, T, topo):
         tt(d, A(p, 128, 256), m, Op.subtract)
         pr, tr = A("PR", 64 * hv, 64 * hv + 64), A("TR", 64 * hv, 64 * hv + 64)
         tt(pr, A("DD", w[0], w[0] + 64), A("DD", w[0] + 64, w[1]), Op.add)
+        sw = A("SW", 64 * hv, 64 * hv + 64)
+        tt(sw, pr, tr, Op.is_gt)
         for b in range(2):
-            tt(A("SWD", w[0] + 64 * b, w[0] + 64 * b + 64), pr, tr, Op.is_gt)
-        tt(A("EE", *w), d, A("SWD", *w), Op.mult)
+            h = (w[0] + 64 * b, w[0] + 64 * b + 64)
+            tt(A("EE", *h), A("DD", *h), sw, Op.mult)
         f = A("F", *w)
         tt(f, A("EE", *w), m, Op.add)
         hi, lo = A("FHI", *w), A("FLO", *w)
         cp(hi, f)
         tt(lo, f, hi, Op.subtract)
-        dmas([("y", ROW("WDS", 0, 2048 * hv, 2048 * hv + 2048), hi), ("y", ROW("WDS", 1, 2048 * hv, 2048 * hv + 2048), lo)])
-        h = A("WDS", 2048 * hv + heads, 2048 * hv + 128, 8)
-        act(h, h, scale=-1.0)
+        if hv:
+            dmas([("y", ROW("WDS", 0, 0, 4096), A("FHI")), ("y", ROW("WDS", 1, 0, 4096), A("FLO"))])
+            h = A("WDS", heads, 256, 8)
+            act(h, h, scale=-1.0)
 
     used, plan = [], []
     for d in sorted([d for d in T.cores if d != core], key=lambda d: len(topo.engines(core, d))):
@@ -442,14 +459,14 @@ def rank_program(g, core, T, topo):
     def slot_scores():
         for c in range(4):
             for m in (2 * c, 2 * c + 1):
-                o, i = A("GS", 1024 * m, 1024 * m + 1024), IND(A("WDS"), A("WL", 64 * m, 64 * m + 64))
+                o, i = A("GS", 256 + 1024 * m, 1280 + 1024 * m), IND(A("WDS"), A("WL", 64 * m, 64 * m + 64))
                 if m & 1:
                     cp(o, i)
                 else:
                     act(o, i)
             p = "P7" if c & 2 else "P6"
             for s in range(16):
-                lo = 2048 * c + s
+                lo = 256 + 2048 * c + s
                 mm(A(p, 128 * (c & 1) + s, 128 * (c & 1) + 128 - 15 + s, 16), A("GS", lo, lo + 2048 - 15, 16), A("RS"))
         for h, p in ((0, "P6"), (1, "P7")):
             w = (256 * h, 256 * h + 256)
@@ -464,7 +481,6 @@ def rank_program(g, core, T, topo):
     def after_exchange(t):
         act(A("HBL"), A("HM%d" % t), Act.Identity, bias=A("LIM", 0, 1))
         for hv in range(2):
-            cp(A("SW", 64 * hv, 64 * hv + 64), A("SWD", 128 * hv, 128 * hv + 64))
             tt(A("DF", 64 * hv, 64 * hv + 64), A("F", 128 * hv, 128 * hv + 64), A("F", 128 * hv + 64, 128 * hv + 128), Op.subtract)
         tt(A("DZ"), A("O", 0, 128), A("O", 128, 256), Op.subtract)
         tt(A("ZS"), A("DZ"), A("SW"), Op.mult)
@@ -507,8 +523,11 @@ def rank_program(g, core, T, topo):
         tt(A("AP"), A("HOLD"), A("CMP", 15, 512, 16), Op.is_gt)
         tt(A("TU"), A("K"), A("W4"), Op.add)
         tt(A("TM"), A("TU"), A("AP"), Op.mult)
-        ts(A("UH"), A("TM"), 2, Op.arith_shift_right, 0x20E8, Op.bitwise_and)
         ts(A("UL"), A("TM"), 2, Op.arith_shift_right, 0x17, Op.bitwise_and)
+        ts(A("UH"), A("TM"), 2, Op.arith_shift_right, 0x20E8, Op.bitwise_and)
+        cp(A("ULB"), A("UL"))
+        for y in range(16):
+            mm(A("P5", 32 * y, 32 * y + 32), A("IB"), A("ULB"))
         cp(A("TT2", 2, 512, 16), A("P3", 0, 32))
         for c in range(4):
             mm(A("P7", 128 * c, 128 * c + 128), A("TT2", 128 * c, 128 * c + 128), A("IB"))
@@ -516,12 +535,10 @@ def rank_program(g, core, T, topo):
         for x in range(16):
             v = 0x2000 + 8 * (x >> 3 & 1) + 128 * (x >> 2 & 1) + 64 * (x >> 1 & 1) + 32 * (x & 1)
             ts(A("AH", 112 + x, 112 + x + 128 * 31 + 1, 128), A("UH"), float(v), Op.is_equal)
-        for y in range(16):
-            v = 16 * (y >> 3 & 1) + (y & 7)
-            ts(A("B0L", 32 * y, 32 * y + 32), A("UL"), float(v), Op.is_equal)
+        tt(A("B0L"), A("P5"), A("YC"), Op.is_equal)
         for j in range(2):
             ts(A("BL", 512 * j, 512 * j + 512), A("B0L"), A("JW%d" % j, 0, 1), Op.mult)
-        for c in range(4):
+        for c in (0, 3, 1, 2):
             mms(A("P1", 64 * c, 64 * c + 64), [(ez("EZ", k), A("MG", 1024 * c + k, 1024 * c + 1024 - 15 + k, 16)) for k in range(16)])
         act(A("T2", 0, 512), A("P7"))
 
@@ -538,33 +555,36 @@ def rank_program(g, core, T, topo):
         for x in range(16):
             mm(A("P7", 0, 16), ez("EZ", x), A("LV", 16 * x, 16 * x + 16), x == 0, x == 15)
         tt(A("E1"), A("NPL" if t == 2 else "NQ"), A("P3", 0, 256), Op.add)
-        ts(A("BT"), A("P5", 0, 256), float(2 ** 23 + 2 ** 19 + 2 ** 15 + 2 ** 11), Op.mult)
         tt(A("DE"), A("E1", 0, 128), A("E1", 128, 256), Op.subtract)
-        ts(A("BT2"), A("BT"), 2 ** 23 + 2 ** 20 + 2 ** 17 + 2 ** 14, Op.bitwise_and)
         tt(A("ES"), A("DE"), A("SW"), Op.mult)
-        tt(A("Y"), A("BT2"), A("P4", 0, 256), Op.add)
         for hv in range(2):
             es = A("ES", 64 * hv, 64 * hv + 64)
             tt(A("E2", 128 * hv, 128 * hv + 64), A("E1", 64 * hv, 64 * hv + 64), es, Op.subtract)
             tt(A("E2", 128 * hv + 64, 128 * hv + 128), A("E1", 128 + 64 * hv, 192 + 64 * hv), es, Op.add)
         ts(A("E3"), A("E2"), 4096.0, Op.min)
         act(A("EHI"), A("E3"))
+        ts(A("BT"), A("P5", 0, 256), float(2 ** 23 + 2 ** 19 + 2 ** 15 + 2 ** 11), Op.mult)
         tt(A("ELO"), A("E3"), A("EHI"), Op.subtract)
-        dmas([("y", ROW("WDE", i, 2048 * hv, 2048 * hv + 2048), A(n, 128 * hv, 128 * hv + 128)) for hv in range(2) for i, n in ((0, "EHI"), (1, "ELO"))])
+        dmas([("y", ROW("WDE", 0, 0, 4096), A("EHI")), ("y", ROW("WDE", 1, 0, 4096), A("ELO"))])
+        ts(A("BT2"), A("BT"), 2 ** 23 + 2 ** 20 + 2 ** 17 + 2 ** 14, Op.bitwise_and)
+        tt(A("Y"), A("BT2"), A("P4", 0, 256), Op.add)
 
     def move_slots(chunks, both=False):
         for m in chunks:
             o, i = A("GE", 256 + 1024 * m, 1280 + 1024 * m), IND(A("WDE"), A("WL", 64 * m, 64 * m + 64))
-            if both and m & 1:
+            if both and m > 4:
                 cp(o, i)
             else:
                 act(o, i)
 
-    def join_slots():
-        scatter(A("GE"), A("SU"), A("AT"))
+    def new_entries():
+        scatter(A("GS"), A("SU"), A("AT"))
 
-    def read_slots(h):
-        mms(A("P5", 256 * h, 256 * h + 256), [(ez("EZ", s), A("GE", 256 + 4096 * h + s, 256 + 4096 * h + 4096 - 15 + s, 16)) for s in range(16)])
+    def clear_entries():
+        dmas([("y", ROW("GS", i, 256 + 2048 * c, 2304 + 2048 * c), (ROW("ZRO", i, 0, 2048)[0], A("ZRO")[1] + A("KK")[1])) for c in range(4) for i in range(2)])
+
+    def read_slots(n, j, start):
+        mms(A("P%d" % (4 + j), 0, 128), [(ez("EZ", s), A(n, 256 + 2048 * j + s, 2304 + 2048 * j - 15 + s, 16)) for s in range(16)], start, not start)
 
     def close_up(j):
         th, d = 2.0 ** (23 - 3 * j), 1 << j
@@ -613,29 +633,39 @@ def rank_program(g, core, T, topo):
         if t:
             lists(t)
             wants()
-            move_slots(range(3, 8))
+            shared_gather()
+            move_slots(range(3, 6))
+            new_entries()
+            for j in range(4):
+                read_slots("GS", j, True)
         minima(0)
         minima(2)
+        shared_clip()
+        if t:
+            move_slots(range(6, 8))
         pair_limits()
         minima(1)
-        decide(0, t)
         if t:
-            join_slots()
-            read_slots(0)
+            read_slots("GE", 0, False)
+            read_slots("GE", 1, False)
+        decide(0, t)
         minima(3)
         if t:
-            read_slots(1)
+            read_slots("GE", 2, False)
+            read_slots("GE", 3, False)
         else:
             slot_windows()
         decide(1, t)
         if t:
-            cp(A("WL"), A("P5"))
+            for j in range(4):
+                cp(A("WL", 128 * j, 128 * j + 128), A("P%d" % (4 + j), 0, 128))
         else:
             late_constants()
         slot_scores()
         roll(t)
         after_exchange(t)
         thresholds(t)
+        clear_entries()
         applicants()
         leave(t)
         logs()
@@ -645,23 +675,34 @@ def rank_program(g, core, T, topo):
         close_up(2)
         close_up(3)
         settle(t)
+        del shared[:]
         if t < 2:
             move_slots(range(3))
 
+    new_entries()
+
+    def read(n, m, start, stop):
+        mms(A("P%d" % m, 0, 64), [(ez("EZ", s), A(n, 256 + 1024 * m + s, 1280 + 1024 * m - 15 + s, 16)) for s in range(16)], start, stop)
+
     move_slots(range(8), True)
-    join_slots()
+    early = (0, 1, 2, 3)
+    for m in early:
+        read("GE", m, True, False)
+    for m in range(8):
+        read("GS", m, m not in early, m in early)
+    for m in (5, 4, 6, 7):
+        read("GE", m, False, True)
     ts(A("OE"), A("O"), 255.5, Op.is_lt, 512.0, Op.mult)
     ts(A("EE"), A("O"), -256.0, Op.add)
     tt(A("YO"), A("EE"), A("OE"), Op.max)
     dmas([("s", nat("YON", c), A("YO", 64 * c, 64 * c + 64)) for c in range(4)])
     dmas([("s", ext(T.yoc[:]), (T.YON[:], [("YON", 0, 1, 1)]))])
     for h in range(2):
-        p = "P%d" % (4 + h)
-        mms(A(p, 0, 256), [(ez("EZ", s), A("GE", 256 + 4096 * h + s, 256 + 4096 * h + 4096 - 15 + s, 16)) for s in range(16)])
-        if h:
-            cp(A("YQ", 256, 512), A(p, 0, 256))
-        else:
-            act(A("YQ", 0, 256), A(p, 0, 256))
+        for m in range(4 * h, 4 * h + 4):
+            if m & 1:
+                cp(A("YQ", 64 * m, 64 * m + 64), A("P%d" % m, 0, 64))
+            else:
+                act(A("YQ", 64 * m, 64 * m + 64), A("P%d" % m, 0, 64))
         dmas([("y", ext(T.yq[:, 256 * h:256 * h + 256]), A("YQ", 256 * h, 256 * h + 256))])
     for s in sorted(cnt):
         if known["g"].get(s, 0) < cnt[s]:

import math
from concourse.bass import DstId, RemoteDMATransfer
from concourse.mybir import dt, AluOpType as Op, ActivationFunctionType as Act

LN2 = math.log(2.0)
BF, F4, FH, I4, U2 = "bfloat16", "float32", "float16", "int32", "uint16"
WIDTH = {}
WHERE = {}
SCRATCH = {}


def _decl(dtype, spec):
    pool, at = "pool_" + dtype, 0
    for item in spec.split():
        n, w = item.split(":")
        WIDTH[n] = int(w)
        WHERE[n] = (pool, at)
        at += (int(w) + 15) // 16 * 16
    SCRATCH[pool] = ("sbuf", [128, at], dtype)


_decl(BF, "XT:4096 WT:768 MT:768 T2:528 WG:4096 D0:4096 D1:4096 MG:4096 ZRO:2112 WDS:4112 WDE:4112 GS:8448 GE:8448 "
          "EZ:144 EZ4:144 EZM:144 EZW:144 INB:128 ULB:32 BO:128 BOP:128 IB:128 IBIG:128 I8K:128 TRI:128 TRQ:128 TRN:128 NLQ:128 NLN:128 "
          "RS:8 RW:8 CADD:64 FHI:256 FLO:256 EHI:256 ELO:256 CMP:512 TT0:512 TT2:512 AH:4336 B0L:512 BL:1024 G2:256 LV:256 AT:256 "
          "CQ:256 CN:256")
_decl(FH, "SH2:128 I16:128 I37:128 IX16:128 C1:256 VF:256 KC0:256 KC1:256 KC2:256 O16:256 O2H:256")
_decl(I4, "OCP:256 QW:512 THI:16 QI:8 KI:8 B1:8 PI:8 T1:256 TQ:256 H:512 HA:512 W1:512 W2:512 W3:512 W6:512 W7:512 W9:512 WSI:32 WSJ:32 TM:32 UH:32 UL:32 PMI:16 BT:256 BT2:256")
_decl(U2, "OU:256 HU:512 PU:16 SU:16 OU2:256 WL:512")
_decl(F4, "IF:128 BOF:128 TA:128 TB:128 TC:128 TD:128 PA:64 PB:64 PG:8 JB:8 BC:8 G0:8 ONE:256 KC:8 KC16:8 KB:8 KW:8 Z0:8 Z1:8 Z4K:8 ODD:8 EVN:8 THF:8 LIM:8 "
          "JW0:8 JW1:8 JW:8 PHF:8 NV16:256 NPL:256 NQ:256 WV:256 HV:256 ATQ:256 ATN:256 JC:16 JD:16 C1F:256 HM0:256 HM1:256 HM2:256 HBL:256 "
          "O:256 OE:256 MN:128 TR:128 MC:256 DD:256 PR:128 SW:128 SWD:256 EE:256 E1:256 DE:128 ES:128 E2:256 E3:256 "
          "F:256 YC:512 SMX:512 PMN:512 RMX:512 RMN:512 R01:512 YN:32 MYK:32 KK:64 K:32 KD:32 KS:512 L4P:32 W4:32 HOLD:32 AP:32 TU:32 LT:128 PEN:128 CK:128 "
          "RK:128 K1:128 K2:128 KM:128 PM:16 PF:16 DZ:128 ZS:128 DF:128 FS:128 F2:256 FL:256 Y:256 MV:272 EQ:256 AC:256 YO:256 YQ:512 "
          "LAND0:128 LAND1:128 LAND2:128")
SCRATCH["OCN"] = ("sbuf", [128, 2, 8, 2, 8], I4)
SCRATCH["YON"] = ("sbuf", [128, 2, 8, 2, 8], F4)
for _i in range(8):
    SCRATCH["P%d" % _i] = ("psum", [128, 512], F4)
    WIDTH["P%d" % _i] = 512
    WHERE["P%d" % _i] = ("P%d" % _i, 0)
SEMAPHORES = (["qv", "qs", "qt", "qg", "sent"] + ["arr%d" % t for t in range(3)] + ["d%d" % i for i in range(30)])


def _bank(name):
    return name[0] == "P" and name[1:].isdigit()


def rank_program(g, core, T, topo):
    rank = T.rank_of(core)
    if rank is None:
        return
    Q = {"v": g.vector, "s": g.scalar, "t": g.tensor, "g": g, "y": g.sync}
    SEM = {"v": "qv", "s": "qs", "t": "qt", "g": "qg"}
    cnt = {}
    known = {q: {} for q in Q}
    snap = {}
    hist = {}

    def A(n, lo=0, hi=None, st=1):
        hi = WIDTH[n] if hi is None else hi
        buf, c0 = WHERE[n]
        ap = T[buf][:, c0 + lo:c0 + hi] if st == 1 else T[buf][:, c0 + lo:c0 + hi:st]
        return (ap, [(n, lo, hi, st)])

    def ROW(n, i, lo, hi):
        buf, c0 = WHERE[n]
        return (T[buf][i:128:16, c0 + lo:c0 + hi], [(n, lo, hi, 1)])

    def IND(win, off):
        return (win[0].indirect(off[0]), win[1] + off[1])

    def clash(a, b):
        if a[1] <= b[0] or b[1] <= a[0]:
            return False
        return (a[0] - b[0]) % math.gcd(a[2], b[2]) == 0

    def need(q, token):
        sem, n = token
        if known[q].get(sem, 0) >= n:
            return
        Q[q].wait_ge(T.sem[sem], n)
        for k2, v2 in snap[token].items():
            if known[q].get(k2, 0) < v2:
                known[q][k2] = v2
        known[q][sem] = n

    def deps(q, reads, writes, dma):
        best = {}
        for regs, wr in ((reads, False), (writes, True)):
            for n, lo, hi, st in regs:
                bank = _bank(n)
                for (r2, tok, q2, w2, d2) in hist.get(n, []):
                    if not (bank and q2 != q):
                        if not clash((lo, hi, st), r2) or not (w2 or wr):
                            continue
                        if q == "t" and q2 == q and tok[1] > cnt.get("qt", 0):
                            continue
                    best[tok[0]] = max(best.get(tok[0], 0), tok[1])
        for s in sorted(best):
            need(q, (s, best[s]))

    def note(q, reads, writes, tok, dma):
        for n, lo, hi, st in reads:
            hist.setdefault(n, []).append(((lo, hi, st), tok, q, False, dma))
        for n, lo, hi, st in writes:
            keep = []
            for h in hist.get(n, []):
                covered = st == 1 and lo <= h[0][0] and h[0][1] <= hi or h[0] == (lo, hi, st)
                if not (covered or _bank(n) and h[2] != q):
                    keep.append(h)
            hist[n] = keep + [((lo, hi, st), tok, q, True, dma)]

    def run(q, call, reads, writes, inc=True):
        deps(q, reads, writes, False)
        sem = SEM[q]
        inst = call()
        tok = (sem, cnt.get(sem, 0) + 1)
        if inc:
            inst.then_inc(T.sem[sem], 1)
            cnt[sem] = tok[1]
            s = dict(known[q])
            s[sem] = tok[1]
            snap[tok] = s
        note(q, reads, writes, tok, False)

    def R(*ops):
        out = []
        for o in ops:
            if isinstance(o, tuple):
                out += o[1]
        return out

    def val(o):
        return o[0] if isinstance(o, tuple) else o

    def tt(o, a, b, op):
        run("v", lambda: g.vector.tensor_tensor(o[0], a[0], b[0], op), R(a, b), o[1])

    def ts(o, a, s1, op0, s2=None, op1=None):
        if op1 is None:
            run("v", lambda: g.vector.tensor_scalar(o[0], a[0], val(s1), None, op0), R(a, s1), o[1])
        else:
            run("v", lambda: g.vector.tensor_scalar(o[0], a[0], val(s1), val(s2), op0, op1), R(a, s1, s2), o[1])

    def cp(o, a):
        run("v", lambda: g.vector.tensor_copy(o[0], a[0]), a[1], o[1])

    def scatter(win, off, a):
        run("v", lambda: g.vector.tensor_copy(win[0].indirect(off[0]), a[0]), R(a, off), win[1])

    def fill(o, c):
        run("v", lambda: g.vector.memset(o[0], c), [], o[1])

    def scan(o, d0, d1, init, op0, op1):
        run("v", lambda: g.vector.tensor_tensor_scan(o[0], d0[0], d1[0], init, op0, op1), R(d0, d1), o[1])

    def act(o, a, func=Act.Copy, bias=0.0, scale=1.0):
        run("s", lambda: g.scalar.activation(o[0], a[0], func, bias=val(bias), scale=val(scale)), R(a, bias, scale), o[1])

    def mm(o, l, r, start=True, stop=True):
        run("t", lambda: g.tensor.matmul(o[0], l[0], r[0], start, stop), R(l, r), o[1], inc=stop)

    def mms(o, pairs, start=True, stop=True):
        for i, (l, r) in enumerate(pairs):
            mm(o, l, r, start and i == 0, stop and i == len(pairs) - 1)

    def iota(o, pattern, base, cm, small=False):
        if small:
            run("g", lambda: g.iota(o[0], pattern, base, cm, allow_small_or_imprecise_dtypes=True), [], o[1])
        else:
            run("g", lambda: g.iota(o[0], pattern, base, cm), [], o[1])

    def aff(o, a, pattern, op, fillv, base, cm):
        run("g", lambda: g.affine_select(o[0], a[0], pattern, op, fillv, base, cm), a[1], o[1])

    ndma = [0]

    def dmas(items):
        sem = "d%d" % ndma[0]
        ndma[0] += 1
        tok = (sem, 16 * len(items))
        allk = {sem: tok[1]}
        for q, o, a in items:
            deps(q, a[1], o[1], True)
            Q[q].dma_start(o[0], a[0]).then_inc(T.sem[sem], 16)
            for k2, v2 in known[q].items():
                allk[k2] = max(allk.get(k2, 0), v2)
        cnt[sem] = tok[1]
        snap[tok] = allk
        for q, o, a in items:
            note(q, a[1], o[1], tok, True)

    def ext(ap, reg=()):
        return (ap, list(reg))

    def nat(n, ck):
        return (T[n][:, ck & 1, :, ck >> 1, :], [(n, 0, 1, 1)])

    dmas([("y", (T.OCN[:], [("OCN", 0, 1, 1)]), ext(T.oc[:]))])
    dmas([("s", A("WT", 256, 768), ext(T.want[:])), ("s", A("THI", 0, 1), ext(T.th[:]))])
    dmas([("y", A("OCP", 64 * c, 64 * c + 64), nat("OCN", c)) for c in range(4)])
    dmas([("y", A("XT", 2048 * c, 2048 * c + 2048), ext(T.x[:, 2048 * c:2048 * c + 2048])) for c in range(2)])
    dmas([("s", A("QW"), ext(T.qs[:]))])

    q1, kc, z0, one = A("QI", 0, 1), A("KC", 0, 1), A("Z0", 0, 1), A("ONE", 0, 128)
    iota(q1, [[0, 1]], 0, 1)
    for c in range(4):
        iota(A("NV16", 64 * c, 64 * c + 64), [[256, 8], [16, 8]], 2048 * (c & 1) + 128 * (c >> 1), 0, True)
    fill(A("ONE"), 1.0)
    fill(A("ZRO"), 0.0)
    for c in range(2):
        act(A("WDS", 2048 * c, 2048 * c + 2048), A("ZRO", 0, 2048))
    aff(A("IF"), one, [[-1, 128]], Op.is_equal, 0.0, 0, 1)
    aff(A("TA"), one, [[-1, 128]], Op.is_equal, 0.0, 1, 1)
    aff(A("TB"), one, [[-16, 8], [0, 16]], Op.is_ge, 0.0, 0, 1)
    aff(A("BOF"), A("TB"), [[16, 8], [0, 16]], Op.is_ge, 0.0, 15, -1)
    aff(A("TD"), A("BOF"), [[1, 128]], Op.is_ge, 0.0, -1, -1)
    aff(A("PG"), A("ONE", 0, 8), [[0, 8]], Op.is_ge, 0.0, -64, 1)
    iota(A("CK"), [[64, 2], [0, 16], [128, 4]], 0, 0, True)
    for c in range(4):
        iota(A("WV", 64 * c, 64 * c + 64), [[1, 64]], 128 * (c & 1) + 64 * (c >> 1), 0, True)
    iota(A("JD"), [[16, 16]], 3840, 0, True)
    iota(A("YC"), [[16, 2], [1, 8], [0, 32]], 0, 0, True)
    fill(A("WT", 0, 256), 0.0)
    fill(A("EZ"), 0.0)
    ts(A("KI", 0, 1), q1, 15, Op.bitwise_and)
    cp(kc, A("KI", 0, 1))
    ts(z0, kc, 0.5, Op.is_lt)
    ts(A("SH2"), A("TA"), 2.0, Op.mult)
    fill(A("SH2", 0, 128, 16), 0.0)
    cp(A("I16"), A("IF"))
    ts(A("I37"), A("IF"), 37.0, Op.mult)
    ts(A("IX16"), A("IF"), 16.0, Op.mult)
    ts(A("NPL"), A("NV16"), kc, Op.add)
    ts(A("C1F"), A("NV16"), 0.125, Op.mult, 512.0, Op.add)
    ts(A("C1"), A("C1F"), z0, Op.mult, -511.0, Op.add)
    ts(A("VF"), A("NV16"), 0.0625, Op.mult)
    ts(A("KC0"), A("ONE"), kc, Op.mult, -1280.0, Op.add)
    act(A("IB"), A("IF"))
    ts(A("OE"), A("OCP"), 511.5, Op.is_lt)
    ts(A("EE"), A("OCP"), 256.0, Op.add)
    tt(A("O"), A("EE"), A("OE"), Op.mult)

    def ez(n, k):
        return A(n, 15 - k, 143 - k)

    def persons():
        cp(A("O16"), A("O"))
        cp(A("OU"), A("O"))

    def lists(t):
        mms(A("P2", 0, 256), [(A("SH2"), A("O16")), (A("I16"), A("C1"))])
        mms(A("P3", 0, 256), [(A("I37"), A("O16")), (A("IX16"), A("VF")), (A("I16"), A("KC%d" % t))])
        for b in range(2):
            mms(A("P3", 256 + 128 * b, 384 + 128 * b),
                [(A("I37"), A("O16", 128 * b, 128 * b + 128)), (A("IX16"), A("VF", 128 - 128 * b, 256 - 128 * b)), (A("I16"), A("KC%d" % t, 0, 128))])
        tt(A("T1"), A("NPL"), A("P2", 0, 256), Op.mult)
        ts(A("TQ"), A("T1"), 4, Op.arith_shift_right)
        tt(A("H", 0, 256), A("TQ"), A("P3", 0, 256), Op.add)
        ts(A("HA", 0, 256), A("H", 0, 256), 4095, Op.bitwise_and)
        cp(A("HU", 0, 256), A("HA", 0, 256))
        for b in range(2):
            tt(A("H", 256 + 128 * b, 384 + 128 * b), A("TQ", 128 - 128 * b, 256 - 128 * b), A("P3", 256 + 128 * b, 384 + 128 * b), Op.add)
        ts(A("HA", 256, 512), A("H", 256, 512), 4095, Op.bitwise_and)
        cp(A("HU", 256, 512), A("HA", 256, 512))

    shared = [3]

    def wants():
        for c in (0, 2, 1, 3):
            act(A("WG", 1024 * c, 1024 * c + 1024), IND(A("WT"), A("OU", 64 * c, 64 * c + 64)))

    def minima(c):
        w = A("WG", 1024 * c, 1024 * c + 1024)
        for j, n in ((0, "D0"), (1, "D1")):
            if j and c in shared:
                continue
            tt(A(n, 1024 * c, 1024 * c + 1024), IND(A("XT"), A("HU", 256 * j + 64 * c, 256 * j + 64 * c + 64)), w, Op.min)
        hv, b3 = c & 1, c >> 1
        for j, n in ((0, "D0"), (1, "D1")):
            o = A("P%d" % hv, 128 * j + 64 * b3, 128 * j + 64 * b3 + 64)
            mm(o, A("IB"), A("CADD"), True, False)
            d = [A(n, 1024 * c + k, 1024 * c + 1024 - 15 + k, 16) for k in range(16)]
            if j and c in shared:
                mms(o, [(ez("EZ4", k), A("WG", 1024 * c + k, 1024 * c + 1024 - 15 + k, 16)) for k in range(16)], False, False)
                mms(o, [(ez("EZM", k), d[k]) for k in range(16)], False, True)
            else:
                mms(o, [(ez("EZ4", k), d[k]) for k in range(16)], False, True)

    def shared_gather():
        for c in shared:
            act(A("D1", 1024 * c, 1024 * c + 1024), IND(A("XT"), A("HU", 256 + 64 * c, 320 + 64 * c)))

    def shared_clip():
        for c in shared:
            for h in range(2):
                w = (1024 * c + 512 * h, 1024 * c + 512 * h + 512)
                mms(A("P%d" % (2 + h)), [(A("IB"), A("WG", *w)), (A("INB"), A("D1", *w))])
                act(A("D1", *w), A("P%d" % (2 + h)), Act.Relu)

    ts(A("PI", 0, 1), q1, 63, Op.bitwise_and)
    cp(A("JB", 0, 1), A("PI", 0, 1))
    fill(A("JB", 1, 2), 63.0 * LN2)
    dmas([("y", A("WDE", 2048 * c, 2048 * c + 2048), A("ZRO", 0, 2048)) for c in range(2)])
    persons()
    lists(0)
    cp(A("EZ", 15, 143, 16), A("BOF", 0, 128, 16))
    fill(A("CADD"), float(7 - rank))
    wants()
    act(A("EZ4"), A("EZ"), scale=4.0)
    act(A("JW", 0, 1), A("JB", 0, 1), Act.Exp, bias=A("JB", 1, 2), scale=-2.0 * LN2)
    act(A("EZM"), A("EZ"), scale=-4.0)
    act(A("INB"), A("IF"), scale=-1.0)
    shared_gather()
    ts(A("KB", 0, 1), kc, 1.5, Op.is_lt)
    for t in (1, 2):
        ts(A("KC%d" % t), A("ONE"), kc, Op.mult, 77.0 * t - 1280.0, Op.add)

    act(A("BO"), A("BOF"))
    act(A("BOP"), A("BOF"), scale=A("KB", 0, 1))
    act(A("TRI"), A("TD"))
    act(A("TRQ"), A("TD"), scale=-256.0)
    act(A("TRN"), A("TD"), scale=-1.0)
    act(A("IBIG"), A("IF"), scale=-33554432.0)
    act(A("I8K"), A("IF"), scale=8192.0)
    for c in range(3):
        w0, w1 = 2048 * c, min(4336, 2048 * c + 2048)
        act(A("AH", w0, w1), A("ZRO", 0, w1 - w0))
    for n in ("TT0", "TT2", "KS"):
        act(A(n), A("ZRO", 0, 512))
    for t in range(3):
        act(A("HM%d" % t), A("ZRO", 0, 256))
    act(A("MV", 256, 272), A("ZRO", 0, 16))
    act(A("T2", 512, 528), A("ZRO", 0, 16))
    act(A("WDS", 4096, 4112), A("ZRO", 0, 16))
    ts(A("Z4K", 0, 1), z0, 4096.0, Op.mult)
    act(A("WDE", 4096, 4112), A("ONE", 0, 16), scale=A("Z4K", 0, 1))
    act(A("NLQ"), A("ZRO", 0, 128))
    act(A("NLN"), A("ZRO", 0, 128))
    ts(A("RS"), A("BOF", 0, 128, 16), A("KB", 0, 1), Op.mult)
    fill(A("RMN"), -1.0e6)
    fill(A("RMN", 0, 512, 16), 1.0e6)
    act(A("RMX"), A("RMN"), scale=-1.0)

    def slot_windows():
        q = A("QW")
        ts(A("H"), q, 256.0, Op.mult)
        ts(A("W1"), q, 4, Op.arith_shift_right, 0x87, Op.bitwise_and)
        ts(A("W2"), q, 5, Op.arith_shift_right, 0x38, Op.bitwise_and)
        ts(A("W3"), q, 1, Op.arith_shift_right, 0x40, Op.bitwise_and)
        ts(A("HA"), A("H"), 0x100F00, Op.bitwise_and)
        tt(A("W6"), A("W1"), A("W2"), Op.add)
        tt(A("W7"), A("W3"), A("HA"), Op.add)
        tt(A("W9"), A("W6"), A("W7"), Op.add)
        ts(A("WL"), A("W9"), 4096.0, Op.min)

    def late_constants():
        ts(A("RW"), A("BOF", 0, 128, 16), kc, Op.mult, 16.0, Op.mult)
        ts(A("G0"), A("BOF", 0, 128, 16), z0, Op.mult)
        cp(A("THF", 0, 1), A("THI", 0, 1))
        ts(A("LIM", 0, 1), A("THF", 0, 1), 4.0, Op.mult, float(rank), Op.add)
        act(A("TA"), one, scale=A("LIM", 0, 1))
        for c in range(4):
            mm(A("P5", 8 * c, 8 * c + 8), A("WT", 256 + 128 * c, 384 + 128 * c), A("RW"))
        mm(A("P4", 0, 8), A("TA"), A("G0"))
        for t in range(3):
            ts(A("HM%d" % t, t, 256, 8), A("ONE", 0, 32), z0, Op.mult, -1.0e6, Op.mult)
        ts(A("WSI"), A("P5", 0, 32), 255.0, Op.add)
        for c in range(4):
            cp(A("L4P", 8 * c, 8 * c + 8), A("P4", 0, 8))
        ts(A("WSJ"), A("WSI"), 255, Op.bitwise_and)
        ts(A("W4"), A("WSJ"), 4.0, Op.mult, 32768.0, Op.add)
        ts(A("KC16", 0, 1), kc, -1.0, Op.mult, 16.0, Op.add)
        ts(A("Z1", 0, 1), kc, 1.0, Op.is_equal)
        fill(A("MT", 0, 256), 131072.0)
        fill(A("R01"), 1.0)
        fill(A("R01", 0, 512, 16), 0.0)
        fill(A("RK"), -1.0e6)
        fill(A("RK", 0, 128, 4), 1.0e6)
        ts(A("CK"), A("CK"), 31.6, Op.add, 2.0 * LN2, Op.mult)
        tt(A("JW1", 0, 1), A("JW", 0, 1), A("PG", 0, 1), Op.mult)
        tt(A("JW0", 0, 1), A("JW", 0, 1), A("JW1", 0, 1), Op.subtract)
        ts(A("PI", 7, 8), q1, 4, Op.arith_shift_right)
        ts(A("PHF", 1, 2), A("PI", 7, 8), 16.0, Op.mult)
        for c in range(4):
            ts(A("TT2", 128 * c, 128 * c + 128, 16), A("ONE", 0, 8), A("PHF", 1, 2), Op.mult, 256.0 + 128.0 * c, Op.add)
        ts(A("TT2", 1, 512, 16), A("ONE", 0, 32), kc, Op.mult)
        ts(A("KW", 0, 1), kc, 2.0, Op.is_equal)
        ts(A("KW", 1, 2), A("KB", 0, 1), 16.0, Op.mult)
        tt(A("KW", 2, 3), A("KW", 0, 1), A("KW", 1, 2), Op.add)
        act(A("EZW"), A("EZ"), scale=A("KW", 2, 3))
        ts(A("JC"), A("JD"), kc, Op.add)
        fill(A("BC", 4, 5), -2000.0 * 63.2 * LN2)
        act(A("NLQ", 0, 128, 16), A("BOF", 0, 128, 16), scale=-256.0)
        act(A("NLN", 1, 128, 16), A("BOF", 0, 128, 16), scale=-1.0)
        ts(A("NQ"), A("ONE"), kc, Op.mult, 256.0, Op.mult)
        tt(A("NQ"), A("NQ"), A("WV"), Op.add)
        ts(A("CQ"), A("WV"), A("Z1", 0, 1), Op.mult)
        ts(A("E2"), A("NV16"), -4096.0, Op.add, z0, Op.mult)
        ts(A("E3"), A("ONE"), A("Z1", 0, 1), Op.mult, 16.0, Op.mult)
        tt(A("CN"), A("E2"), A("E3"), Op.add)
        for x in range(16):
            mm(A("P4", x, 256 - 15 + x, 16), A("IB"), A("CQ", 16 * x, 16 * x + 16))
        for x in range(16):
            mm(A("P5", x, 256 - 15 + x, 16), A("IB"), A("CN", 16 * x, 16 * x + 16))
        act(A("ATQ"), A("P4", 0, 256))
        act(A("ATN"), A("P5", 0, 256))

    def pair_limits():
        tt(A("MN"), A("O", 0, 128), A("O", 128, 256), Op.min)
        ts(A("TR"), A("MN"), 255.5, Op.is_lt, 1.0e6, Op.mult)

    def decide(hv, heads):
        p = "P%d" % hv
        w = (128 * hv, 128 * hv + 128)
        m, d = A("MC", *w), A("DD", *w)
        cp(m, A(p, 0, 128))
        tt(d, A(p, 128, 256), m, Op.subtract)
        pr, tr = A("PR", 64 * hv, 64 * hv + 64), A("TR", 64 * hv, 64 * hv + 64)
        tt(pr, A("DD", w[0], w[0] + 64), A("DD", w[0] + 64, w[1]), Op.add)
        sw = A("SW", 64 * hv, 64 * hv + 64)
        tt(sw, pr, tr, Op.is_gt)
        for b in range(2):
            h = (w[0] + 64 * b, w[0] + 64 * b + 64)
            tt(A("EE", *h), A("DD", *h), sw, Op.mult)
        f = A("F", *w)
        tt(f, A("EE", *w), m, Op.add)
        hi, lo = A("FHI", *w), A("FLO", *w)
        cp(hi, f)
        tt(lo, f, hi, Op.subtract)
        if hv:
            dmas([("y", ROW("WDS", 0, 0, 4096), A("FHI")), ("y", ROW("WDS", 1, 0, 4096), A("FLO"))])
            h = A("WDS", heads, 256, 8)
            act(h, h, scale=-1.0)

    used, plan = [], []
    for d in sorted([d for d in T.cores if d != core], key=lambda d: len(topo.engines(core, d))):
        es = [e for e in topo.engines(core, d) if e not in used][:4]
        used += es
        plan.append((d, sum(1 << e for e in es), len(es)))

    def send(t):
        own, reg = A("LAND%d" % t, 32 * rank, 32 * rank + 32)
        deps("g", reg, [], True)
        tr = []
        for d, mask, ne in plan:
            rid, pid = topo.addr(d, core)
            tr.append(RemoteDMATransfer(dst_ids=[DstId(rid=rid, pnc=pid)], dma_engine_mask=mask, remote_sem=T.sem["arr%d" % t], src=own, dst=own))
        g.remote_dma_fused(tr, local_sem=T.sem.sent)
        n = sum([p[2] for p in plan])
        cnt["sent"] = cnt.get("sent", 0) + n
        tok = ("arr%d" % t, n)
        cnt[tok[0]] = n
        snap[tok] = {tok[0]: n}
        for r in range(4):
            if r != rank:
                hist.setdefault("LAND%d" % t, []).append(((32 * r, 32 * r + 32, 1), tok, "net", True, True))

    def slot_scores():
        for c in range(4):
            for m in (2 * c, 2 * c + 1):
                o, i = A("GS", 256 + 1024 * m, 1280 + 1024 * m), IND(A("WDS"), A("WL", 64 * m, 64 * m + 64))
                if m & 1:
                    cp(o, i)
                else:
                    act(o, i)
            p = "P7" if c & 2 else "P6"
            for s in range(16):
                lo = 256 + 2048 * c + s
                mm(A(p, 128 * (c & 1) + s, 128 * (c & 1) + 128 - 15 + s, 16), A("GS", lo, lo + 2048 - 15, 16), A("RS"))
        for h, p in ((0, "P6"), (1, "P7")):
            w = (256 * h, 256 * h + 256)
            scan(A("PMN", *w), A("RMN", 0, 256), A(p, 0, 256), 0.0, Op.max, Op.min)
            scan(A("SMX", *w), A("RMX", 0, 256), A(p, 0, 256), 0.0, Op.min, Op.max)

    def roll(t):
        ts(A("YN"), A("PMN", 15, 512, 16), -1.0, Op.mult)
        tt(A("LAND%d" % t, 32 * rank, 32 * rank + 32), A("YN"), A("SMX", 15, 512, 16), Op.max)
        send(t)

    def after_exchange(t):
        act(A("HBL"), A("HM%d" % t), Act.Identity, bias=A("LIM", 0, 1))
        for hv in range(2):
            tt(A("DF", 64 * hv, 64 * hv + 64), A("F", 128 * hv, 128 * hv + 64), A("F", 128 * hv + 64, 128 * hv + 128), Op.subtract)
        tt(A("DZ"), A("O", 0, 128), A("O", 128, 256), Op.subtract)
        tt(A("ZS"), A("DZ"), A("SW"), Op.mult)
        tt(A("FS"), A("DF"), A("SW"), Op.mult)
        tt(A("O2H", 0, 128), A("O", 0, 128), A("ZS"), Op.subtract)
        tt(A("O2H", 128, 256), A("O", 128, 256), A("ZS"), Op.add)
        cp(A("OU2"), A("O2H"))
        for hv in range(2):
            tt(A("F2", 64 * hv, 64 * hv + 64), A("F", 128 * hv, 128 * hv + 64), A("FS", 64 * hv, 64 * hv + 64), Op.subtract)
            tt(A("F2", 128 + 64 * hv, 192 + 64 * hv), A("F", 128 * hv + 64, 128 * hv + 128), A("FS", 64 * hv, 64 * hv + 64), Op.add)
        tt(A("FL"), A("F2"), A("HBL"), Op.add)
        ts(A("MYK"), A("LAND%d" % t, 32 * rank, 32 * rank + 32), 0.5, Op.max)

    def place_keys(c, vec):
        o, i = A("MG", 1024 * c, 1024 * c + 1024), IND(A("MT"), A("OU2", 64 * c, 64 * c + 64))
        if vec:
            cp(o, i)
        else:
            act(o, i)

    def thresholds(t):
        ld = "LAND%d" % t
        tt(A("KK"), A(ld, 0, 64), A(ld, 64, 128), Op.max)
        tt(A("K"), A("KK", 0, 32), A("KK", 32, 64), Op.max)
        cp(A("TT0", 0, 512, 16), A("K"))
        tt(A("TT0", 1, 512, 16), A("K"), A("TT0", 0, 512, 16), Op.subtract)
        for c in range(4):
            mm(A("P0", 128 * c, 128 * c + 128), A("TT0", 128 * c, 128 * c + 128), A("IB"))
        act(A("MT", 256, 768), A("P0"))
        for c in range(3):
            place_keys(c, False)

    def applicants():
        tt(A("KD"), A("K"), A("L4P"), Op.subtract)
        ts(A("KS", 0, 512, 16), A("KD"), 1.0, Op.max)
        scan(A("P2"), A("R01"), A("KS"), 0.0, Op.mult, Op.add)
        tt(A("CMP"), A("PMN"), A("P2"), Op.is_ge)
        mms(A("P3", 0, 32), [(A("IB"), A("CMP", s, 512 - 15 + s, 16)) for s in range(16)])
        tt(A("HOLD"), A("K"), A("MYK"), Op.is_equal)
        tt(A("AP"), A("HOLD"), A("CMP", 15, 512, 16), Op.is_gt)
        tt(A("TU"), A("K"), A("W4"), Op.add)
        tt(A("TM"), A("TU"), A("AP"), Op.mult)
        ts(A("UL"), A("TM"), 2, Op.arith_shift_right, 0x17, Op.bitwise_and)
        ts(A("UH"), A("TM"), 2, Op.arith_shift_right, 0x20E8, Op.bitwise_and)
        cp(A("ULB"), A("UL"))
        for y in range(16):
            mm(A("P5", 32 * y, 32 * y + 32), A("IB"), A("ULB"))
        cp(A("TT2", 2, 512, 16), A("P3", 0, 32))
        for c in range(4):
            mm(A("P7", 128 * c, 128 * c + 128), A("TT2", 128 * c, 128 * c + 128), A("IB"))
        place_keys(3, True)
        for x in range(16):
            v = 0x2000 + 8 * (x >> 3 & 1) + 128 * (x >> 2 & 1) + 64 * (x >> 1 & 1) + 32 * (x & 1)
            ts(A("AH", 112 + x, 112 + x + 128 * 31 + 1, 128), A("UH"), float(v), Op.is_equal)
        tt(A("B0L"), A("P5"), A("YC"), Op.is_equal)
        for j in range(2):
            ts(A("BL", 512 * j, 512 * j + 512), A("B0L"), A("JW%d" % j, 0, 1), Op.mult)
        for c in (0, 3, 1, 2):
            mms(A("P1", 64 * c, 64 * c + 64), [(ez("EZ", k), A("MG", 1024 * c + k, 1024 * c + 1024 - 15 + k, 16)) for k in range(16)])
        act(A("T2", 0, 512), A("P7"))

    def leave(t):
        tt(A("LV"), A("FL"), A("P1", 0, 256), Op.is_lt)
        mms(A("P3", 0, 256), [(A("TRN" if t == 2 else "TRQ"), A("LV")), (A("I8K"), A("LV"))])
        for h in range(2):
            mm(A("P5", 128 * h, 128 * h + 128), A("LV", 128 * h, 128 * h + 128), A("TRI"))
        for h in range(2):
            mms(A("P4", 128 * h, 128 * h + 128), [(A("O2H", 128 * h, 128 * h + 128), A("I16")), (A("LV", 128 * h, 128 * h + 128), A("IBIG"))])
        mm(A("P2", 0, 256), A("BO"), A("LV"))
        for x in range(16):
            mm(A("P2", 256 + x, 512 - 15 + x, 16), A("NLN" if t == 2 else "NLQ"), A("LV", 16 * x, 16 * x + 16))
        for x in range(16):
            mm(A("P7", 0, 16), ez("EZ", x), A("LV", 16 * x, 16 * x + 16), x == 0, x == 15)
        tt(A("E1"), A("NPL" if t == 2 else "NQ"), A("P3", 0, 256), Op.add)
        tt(A("DE"), A("E1", 0, 128), A("E1", 128, 256), Op.subtract)
        tt(A("ES"), A("DE"), A("SW"), Op.mult)
        for hv in range(2):
            es = A("ES", 64 * hv, 64 * hv + 64)
            tt(A("E2", 128 * hv, 128 * hv + 64), A("E1", 64 * hv, 64 * hv + 64), es, Op.subtract)
            tt(A("E2", 128 * hv + 64, 128 * hv + 128), A("E1", 128 + 64 * hv, 192 + 64 * hv), es, Op.add)
        ts(A("E3"), A("E2"), 4096.0, Op.min)
        act(A("EHI"), A("E3"))
        ts(A("BT"), A("P5", 0, 256), float(2 ** 23 + 2 ** 19 + 2 ** 15 + 2 ** 11), Op.mult)
        tt(A("ELO"), A("E3"), A("EHI"), Op.subtract)
        dmas([("y", ROW("WDE", 0, 0, 4096), A("EHI")), ("y", ROW("WDE", 1, 0, 4096), A("ELO"))])
        ts(A("BT2"), A("BT"), 2 ** 23 + 2 ** 20 + 2 ** 17 + 2 ** 14, Op.bitwise_and)
        tt(A("Y"), A("BT2"), A("P4", 0, 256), Op.add)

    def move_slots(chunks, both=False):
        for m in chunks:
            o, i = A("GE", 256 + 1024 * m, 1280 + 1024 * m), IND(A("WDE"), A("WL", 64 * m, 64 * m + 64))
            if both and m > 4:
                cp(o, i)
            else:
                act(o, i)

    def new_entries():
        scatter(A("GS"), A("SU"), A("AT"))

    def clear_entries():
        dmas([("y", ROW("GS", i, 256 + 2048 * c, 2304 + 2048 * c), (ROW("ZRO", i, 0, 2048)[0], A("ZRO")[1] + A("KK")[1])) for c in range(4) for i in range(2)])

    def read_slots(n, j, start):
        mms(A("P%d" % (4 + j), 0, 128), [(ez("EZ", s), A(n, 256 + 2048 * j + s, 2304 + 2048 * j - 15 + s, 16)) for s in range(16)], start, not start)

    def close_up(j):
        th, d = 2.0 ** (23 - 3 * j), 1 << j
        ts(A("P5", 0, 256), A("Y"), th, Op.is_lt)
        ts(A("MV", 0, 256), A("Y"), th, Op.subtract, 0.0, Op.max)
        tt(A("P5", 256, 512), A("Y"), A("P5", 0, 256), Op.mult)
        tt(A("Y"), A("P5", 256, 512), A("MV", d, 256 + d), Op.max)

    def logs():
        for c in range(4):
            for h in range(8):
                cg = 8 * c + h
                w0 = 112 + 128 * cg - 16 * h
                mm(A("P6", c, 128 - 3 + c, 4), A("AH", w0, w0 + 128), A("BL", cg, 1024 - 31 + cg, 32), h == 0, h == 7)
        act(A("LT"), A("P6", 0, 128), Act.Ln, bias=2.0 ** -64)
        act(A("PEN"), A("LT"), Act.Relu, bias=A("BC", 4, 5), scale=-2000.0)

    def winners(t):
        tt(A("K1"), A("CK"), A("LT"), Op.subtract)
        tt(A("K2"), A("K1"), A("PEN"), Op.add)
        scan(A("KM"), A("RK"), A("K2"), 0.0, Op.max, Op.min)
        tt(A("PM"), A("KM", 3, 64, 4), A("KM", 67, 128, 4), Op.min)
        ts(A("PF"), A("P7", 0, 16), 0.5, Op.is_lt, 1.0e4, Op.mult)
        tt(A("PM"), A("PM"), A("PF"), Op.max)
        ts(A("PMI"), A("PM"), 0.5 / LN2, Op.mult, 512.0, Op.min)
        cp(A("PU"), A("PMI"))
        act(A("G2"), IND(A("T2"), A("PU")))
        for x in range(16):
            mm(A("P6", 16 * x, 16 * x + 16), A("BOP"), A("G2", x, 256 - 15 + x, 16))
        for x in range(16):
            mm(A("P6", 256, 272), ez("EZW", x), A("G2", x, 256 - 15 + x, 16), x == 0, x == 15)

    def settle(t):
        for h in range(2):
            mm(A("P1", 128 * h, 128 * h + 128), A("Y", 128 * h, 128 * h + 128), A("IF"))
        ts(A("EQ"), A("P2", 0, 256), A("KC16", 0, 1), Op.is_equal)
        tt(A("AC"), A("EQ"), A("P6", 0, 256), Op.mult)
        tt(A("O"), A("P1", 0, 256), A("AC"), Op.max)
        if t < 2:
            persons()
        tt(A("JD"), A("P6", 256, 272), A("JC"), Op.max)
        ts(A("SU"), A("JD"), -3840.0, Op.add)
        tt(A("AT"), A("ATN" if t == 2 else "ATQ"), A("P2", 256, 512), Op.add)

    for t in range(3):
        if t:
            lists(t)
            wants()
            shared_gather()
            move_slots(range(3, 6))
            new_entries()
            for j in range(4):
                read_slots("GS", j, True)
        minima(0)
        minima(2)
        shared_clip()
        if t:
            move_slots(range(6, 8))
        pair_limits()
        minima(1)
        if t:
            read_slots("GE", 0, False)
            read_slots("GE", 1, False)
        decide(0, t)
        minima(3)
        if t:
            read_slots("GE", 2, False)
            read_slots("GE", 3, False)
        else:
            slot_windows()
        decide(1, t)
        if t:
            for j in range(4):
                cp(A("WL", 128 * j, 128 * j + 128), A("P%d" % (4 + j), 0, 128))
        else:
            late_constants()
        slot_scores()
        roll(t)
        after_exchange(t)
        thresholds(t)
        clear_entries()
        applicants()
        leave(t)
        logs()
        close_up(0)
        close_up(1)
        winners(t)
        close_up(2)
        close_up(3)
        settle(t)
        del shared[:]
        if t < 2:
            move_slots(range(3))

    new_entries()

    def read(n, m, start, stop):
        mms(A("P%d" % m, 0, 64), [(ez("EZ", s), A(n, 256 + 1024 * m + s, 1280 + 1024 * m - 15 + s, 16)) for s in range(16)], start, stop)

    move_slots(range(8), True)
    early = (0, 1, 2, 3)
    for m in early:
        read("GE", m, True, False)
    for m in range(8):
        read("GS", m, m not in early, m in early)
    for m in (5, 4, 6, 7):
        read("GE", m, False, True)
    ts(A("OE"), A("O"), 255.5, Op.is_lt, 512.0, Op.mult)
    ts(A("EE"), A("O"), -256.0, Op.add)
    tt(A("YO"), A("EE"), A("OE"), Op.max)
    dmas([("s", nat("YON", c), A("YO", 64 * c, 64 * c + 64)) for c in range(4)])
    dmas([("s", ext(T.yoc[:]), (T.YON[:], [("YON", 0, 1, 1)]))])
    for h in range(2):
        for m in range(4 * h, 4 * h + 4):
            if m & 1:
                cp(A("YQ", 64 * m, 64 * m + 64), A("P%d" % m, 0, 64))
            else:
                act(A("YQ", 64 * m, 64 * m + 64), A("P%d" % m, 0, 64))
        dmas([("y", ext(T.yq[:, 256 * h:256 * h + 256]), A("YQ", 256 * h, 256 * h + 256))])
    for s in sorted(cnt):
        if known["g"].get(s, 0) < cnt[s]:
            g.wait_ge(T.sem[s], cnt[s])
